import numpy as np
import ml_dtypes


def mxq(x, axis, fmt="e4m3"):
    dtype, down = {"e4m3": (ml_dtypes.float8_e4m3fn, 7), "e5m2": (ml_dtypes.float8_e5m2, 14)}[fmt]
    v = np.moveaxis(np.asarray(x, np.float32).astype(ml_dtypes.bfloat16).astype(np.float64), axis, -1)
    blocks = v.reshape(v.shape[:-1] + (-1, 32))
    amax = np.abs(blocks).max(-1, keepdims=True)
    byte = np.maximum(np.where(amax > 0, np.frexp(amax)[1] - 1 + 127, 0) - down, 1)
    scale = np.exp2(byte - 127.0)
    codes = (blocks / scale).astype(np.float32).astype(dtype).astype(np.float64)
    return np.moveaxis((codes * scale).reshape(v.shape), -1, axis)


WIDE = False


def mx_kscale(k):
    if not WIDE:
        return np.ones(k)
    levels = np.array([10, -10, 5, -5, 0])
    if k % 512:
        return np.exp2(np.random.permutation(np.resize(levels, k // 32))).repeat(32)
    a = np.empty((k // 512, 16))
    for p in range(k // 512):
        a[p, :8] = np.random.permutation(np.resize(levels, 8))
        for g in range(8):
            far = levels[np.abs(levels - a[p, g]) >= 10]
            a[p, g + 8] = far[np.random.randint(len(far))]
    return np.exp2(a.ravel()).repeat(32)


def f64(x):
    return np.asarray(x).astype(np.float64)


def striped(idx):
    return np.tile(idx.reshape(-1, 16).T, (8, 1)).astype(np.uint16)


def unstriped(offs):
    return offs[:16].T.reshape(-1).astype(np.int64)


E2M1 = np.array([0.0, 0.5, 1.0, 1.5, 2.0, 3.0, 4.0, 6.0, -0.0, -0.5, -1.0, -1.5, -2.0, -3.0, -4.0, -6.0])


def pack_weight(w, fmt):
    k, n = w.shape
    w = f64(np.asarray(w, np.float32).astype(ml_dtypes.bfloat16)).reshape(k // 32, 32, n)
    amax = np.abs(w).max(1)
    if fmt == "e4m3":
        byte = np.frexp(amax)[1] - 1 + 127 - 7
    else:
        mant, ex = np.frexp(amax / 6.0)
        byte = np.where(mant > 0.5, ex, ex - 1) + 127
    byte = np.clip(np.where(amax > 0, byte, 1), 1, 254)
    scaled = (w * np.exp2(127.0 - byte)[:, None, :]).reshape(k, n).astype(np.float32)
    by_word = np.ascontiguousarray(scaled.reshape(k // 512, 128, 4, n).transpose(0, 1, 3, 2))
    if fmt == "e4m3":
        words = by_word.astype(ml_dtypes.float8_e4m3fn).view(np.uint8)
    else:
        c = by_word.astype(ml_dtypes.float4_e2m1fn).view(np.uint8) & 0xF
        words = (c[..., 0::2] | (c[..., 1::2] << 4)).reshape(k // 512, 128, 2 * n)
    return np.ascontiguousarray(words), np.ascontiguousarray(byte.astype(np.uint8).reshape(k // 512, 16, n))


def unpack_weight(words, scales, fmt):
    g, _, n = scales.shape
    words = np.ascontiguousarray(words).reshape(g, 128, n, -1)
    if fmt == "e4m3":
        vals = words.view(ml_dtypes.float8_e4m3fn).astype(np.float64)
    else:
        nib = np.empty((g, 128, n, 4), np.uint8)
        nib[..., 0::2] = words & 0xF
        nib[..., 1::2] = words >> 4
        vals = E2M1[nib]
    vals = vals * np.repeat(np.exp2(scales.astype(np.float64) - 127.0), 8, axis=1)[..., None]
    return vals.transpose(0, 1, 3, 2).reshape(g * 512, n)


def gelu(v):
    return 0.5 * v * (1.0 + np.tanh(np.sqrt(2.0 / np.pi) * (v + 0.044715 * v**3)))


K, T, S, P, H, N = 1024, 4096, 1024, 512, 512, 384

def setup_inputs():
    n = np.random.standard_normal
    s = mx_kscale(K)[:, None]
    u = mx_kscale(H)[:, None]
    tab_words, tab_scales = pack_weight(n((K, T)) * s, "e4m3")
    w2_words, w2_scales = pack_weight(n((H, H)) / np.sqrt(H) / u, "e2m1")
    w4_words, w4_scales = pack_weight(1.2 * n((K, N)) / np.sqrt(K) / s, "e4m3")
    perm = np.random.permutation(S)
    return {
        "tab_words": tab_words, "tab_scales": tab_scales,
        "offs": striped(np.random.permutation(T)[:S]),
        "pos1": striped(perm[:P]),
        "pos2": striped(perm[P:]),
        "w1": (0.53 * n((K, H)) / np.sqrt(K) / s).astype(np.float32),
        "w2_words": w2_words, "w2_scales": w2_scales,
        "w3": (n((H, N)) / np.sqrt(H) / u).astype(np.float32),
        "w4_words": w4_words, "w4_scales": w4_scales,
        "swing": (np.random.uniform(1.2, 3.2, H) * u[:, 0]).astype(np.float32),
        "slope": np.random.uniform(1, 3, H).astype(np.float32),
        "share": np.random.uniform(0.1, 0.5, H).astype(np.float32),
        "leaf": (2.0 * n((H, P))).astype(np.float32),
        "skip": np.random.uniform(0.5, 1.5, H).astype(np.float32),
        "wgs": np.exp(0.3 * n((128, P))).astype(np.float32),
        "gain": (np.random.uniform(0.5, 2.0, H) * u[:, 0]).astype(np.float32),
    }

def reference(tab_words, tab_scales, offs, pos1, pos2, w1, w2_words, w2_scales, w3, w4_words, w4_scales,
              swing, slope, share, leaf, skip, wgs, gain):
    v = unpack_weight(tab_words, tab_scales, "e4m3")[:, unstriped(offs)]
    raw = mxq(f64(w1), 0, "e4m3").T @ v
    f = f64(swing)[:, None] * np.sin(raw)
    e = unpack_weight(w2_words, w2_scales, "e2m1").T @ mxq(f, 0, "e4m3")
    h = np.maximum(raw, e)
    top = h.max(axis=1)
    look = 1.0 / (1.0 + np.exp(-f64(slope)[:, None] * (h[:, unstriped(pos1)] - f64(share)[:, None] * top[:, None])))
    a = look * f64(leaf)
    page = f64(skip)[:, None] * h
    page[:, unstriped(pos2)] = np.tile(f64(wgs), (H // 128, 1)) * a
    y = mxq(f64(w3), 0, "e4m3").T @ mxq(f64(gain)[:, None] * page, 0, "e4m3")
    d = unpack_weight(w4_words, w4_scales, "e4m3").T @ v
    return np.maximum(y, np.tanh(d))

@@ -1,0 +1,288 @@
+from contextlib import ExitStack
+
+import concourse.mybir as mybir
+
+K, T, S, L, H, N = 1024, 4096, 1024, 512, 512, 384
+FLOPS = 2 * S * (K * H + H * H + H * N + K * N)
+
+F32 = mybir.dt.float32
+BF16 = mybir.dt.bfloat16
+I32 = mybir.dt.int32
+U32 = mybir.dt.uint32
+U16 = mybir.dt.uint16
+U8 = mybir.dt.uint8
+FP8X4 = mybir.dt.float8_e4m3fn_x4
+FP4X4 = mybir.dt.float4_e2m1fn_x4
+ALU = mybir.AluOpType
+ACT = mybir.ActivationFunctionType
+AX = mybir.AxisListType
+
+P = 128
+PACK = 4
+HALF = 512
+PASSES = K // (P * PACK)
+TILES = N // P
+QUARTER = 256
+
+
+def weave(src):
+    return src.rearrange("p t (c i) -> p c t i", i=4)
+
+
+def woven(dst):
+    return dst.rearrange("p (c i t) -> p c t i", i=4, t=PACK)
+
+
+def tile_list_onion_neck_features_kernel(
+    tc, tab_words, tab_scales, offs, pos1, pos2, w1, w2_words, w2_scales, w3, w4_words, w4_scales,
+    swing, slope, share, leaf, skip, wgs, gain, out,
+):
+    nc = tc.nc
+    with ExitStack() as ctx:
+        lists = ctx.enter_context(tc.tile_pool(name="lists", bufs=1))
+        keep = ctx.enter_context(tc.tile_pool(name="keep", bufs=1))
+        ring = ctx.enter_context(tc.tile_pool(name="ring", bufs=3))
+        rows = ctx.enter_context(tc.tile_pool(name="rows", bufs=4))
+        psum = ctx.enter_context(tc.psum_pool(name="psum", bufs=1))
+
+        def held(name, shape, dtype):
+            return keep.tile(shape, dtype, name=name, align_bytes=64)
+
+        def bank(b):
+            return psum.tile([P, HALF], F32, name="bank%d" % b, tag="bank%d" % b)
+
+        def by_row(name, vec, queue):
+            tile = held(name, [P, PACK], F32)
+            queue.dma_start(out=tile[:], in_=vec.rearrange("(p t) -> p t", t=PACK))
+            return tile
+
+        idx = lists.tile([P, S // 16], U16, name="idx")
+        p1 = lists.tile([P, L // 16], U16, name="p1")
+        p2 = lists.tile([P, L // 16], U16, name="p2")
+        nc.sync.dma_start(idx[:], offs)
+
+        tab_s = held("tab_s", [P, T], U8)
+        nc.vector.memset(tab_s[:].bitcast(I32), 0)
+        w2_s_in = held("w2_s_in", [P, H], U8)
+        nc.vector.memset(w2_s_in[:].bitcast(I32), 0)
+        w4_s = held("w4_s", [P, N], U8)
+        nc.vector.memset(w4_s[:].bitcast(I32), 0)
+        for q in range(4):
+            nc.gpsimd.dma_start(out=tab_s[32 * q : 32 * q + 8, :].bitcast(I32),
+                                in_=tab_scales[:, 4 * q : 4 * q + 4, :].bitcast(I32))
+        for q in range(4):
+            nc.gpsimd.dma_start(out=w2_s_in[32 * q : 32 * q + 4, :].bitcast(I32),
+                                in_=w2_scales[0, 4 * q : 4 * q + 4, :].bitcast(I32))
+
+        swing_t = by_row("swing_t", swing, nc.scalar)
+        w2_in = held("w2_in", [P, 2 * H], U8)
+        nc.scalar.dma_start(out=w2_in[:].bitcast(I32), in_=w2_words[0].bitcast(I32))
+
+        w1_in = []
+        for a in range(PASSES):
+            tile = held("w1_in%d" % a, [P, PACK, H], F32)
+            nc.sync.dma_start(out=tile[:], in_=w1[512 * a : 512 * (a + 1), :].rearrange("(p j) c -> p j c", j=PACK))
+            w1_in.append(tile)
+        tab_w = []
+        for a in range(PASSES):
+            tile = held("tab_w%d" % a, [P, T], U32)
+            nc.sync.dma_start(out=tile[:].bitcast(I32), in_=tab_words[a].rearrange("p c i -> p (c i)").bitcast(I32))
+            tab_w.append(tile)
+        skip_t = by_row("skip_t", skip, nc.sync)
+        w3_in = held("w3_in", [P, PACK, N], F32)
+        nc.sync.dma_start(out=w3_in[:], in_=w3.rearrange("(p j) c -> p j c", j=PACK))
+        leaf_t = held("leaf_t", [P, PACK * L], F32)
+        nc.sync.dma_start(out=leaf_t[:], in_=leaf.rearrange("(p t) m -> p (t m)", t=PACK))
+        wgs_t = held("wgs_t", [P, PACK * L], F32)
+        for q in (0, 2, 1, 3):
+            nc.sync.dma_start(out=wgs_t[32 * q : 32 * (q + 1), :], in_=wgs.rearrange("(p t) m -> p (t m)", t=PACK))
+        w4_w = held("w4_w", [P, PASSES, N], U32)
+        nc.sync.dma_start(out=w4_w[:].bitcast(I32), in_=w4_words.rearrange("a p c i -> p a (c i)").bitcast(I32))
+        for q in range(4):
+            nc.sync.dma_start(out=w4_s[32 * q : 32 * q + 8, :].bitcast(I32),
+                              in_=w4_scales[:, 4 * q : 4 * q + 4, :].bitcast(I32))
+        nc.sync.dma_start(p1[:], pos1)
+        nc.sync.dma_start(p2[:], pos2)
+        slope_t = by_row("slope_t", slope, nc.sync)
+        share_t = by_row("share_t", share, nc.sync)
+        gain_t = by_row("gain_t", gain, nc.sync)
+
+        third = held("third", [P, PACK], F32)
+        nc.vector.tensor_scalar(out=third[:], in0=swing_t[:], scalar1=0.0, scalar2=None, op0=ALU.is_ge)
+        size = held("size", [P, PACK], F32)
+        nc.vector.scalar_tensor_tensor(out=size[:], in0=swing_t[:], scalar=-1.0, in1=swing_t[:], op0=ALU.mult, op1=ALU.max)
+        nc.vector.tensor_scalar(out=third[:], in0=third[:], scalar1=-2.0 / 3.0, scalar2=1.0 / 3.0, op0=ALU.mult, op1=ALU.add)
+        root = held("root", [P, PACK], F32)
+        nc.scalar.activation(out=root[:], in_=size[:], func=ACT.Sqrt, scale=4.0)
+        triple = held("triple", [P, PACK], F32)
+        nc.vector.tensor_scalar(out=triple[:], in0=size[:], scalar1=3.0, scalar2=None, op0=ALU.mult)
+
+        w2_w = held("w2_w", [P, 2 * H], U8)
+        nc.vector.tensor_copy(out=w2_w[:].rearrange("p (t m b) -> p m t b", t=PACK, b=2),
+                              in_=w2_in[:].rearrange("p (m t b) -> p m t b", t=PACK, b=2))
+
+        w2_s = held("w2_s", [P, H], U8)
+        nc.gpsimd.tensor_copy(out=w2_s[:].rearrange("p (t m) -> p m t", t=PACK),
+                              in_=w2_s_in[:].rearrange("p (m t) -> p m t", t=PACK))
+
+        w1_w, w1_s = [], []
+        for a in range(PASSES):
+            grouped = held("w1_g%d" % a, [P, PACK * H], BF16)
+            nc.scalar.copy(out=grouped[:].rearrange("p (t m j) -> p m j t", t=PACK, j=PACK),
+                           in_=w1_in[a][:].rearrange("p j (m t) -> p m j t", t=PACK))
+            words = held("w1_w%d" % a, [P, H], U32)
+            scales = held("w1_s%d" % a, [P, H], U8)
+            nc.vector.quantize_mx(out=words[:].bitcast(FP8X4), scales=scales[:], in_=grouped[:])
+            w1_w.append(words)
+            w1_s.append(scales)
+
+        v_s = held("v_s", [P, S], U8)
+        nc.vector.tensor_copy(out=v_s[:], in_=tab_s[:].indirect(idx[:]))
+        v_w = {}
+
+        def gather(a, c):
+            tile = held("v_w%d%d" % (a, c), [P, HALF], U32)
+            nc.vector.tensor_copy(out=tile[:], in_=tab_w[a][:].indirect(idx[:, 32 * c : 32 * (c + 1)]))
+            v_w[a, c] = tile
+
+        def on_table(acc, words, scales, a, c):
+            nc.tensor.matmul_mx(out=acc[:], lhsT=words.bitcast(FP8X4), lhsT_scale=scales,
+                                rhs=v_w[a, c][:].bitcast(FP8X4), rhs_scale=v_s[4 * a : P, HALF * c : HALF * (c + 1)],
+                                start=(a == 0), stop=(a == PASSES - 1))
+
+        raw_ps = {(c, t): bank(PACK * c + t) for c in range(2) for t in range(PACK)}
+        for a in range(PASSES):
+            for c in range(2):
+                gather(a, c)
+                for t in range(PACK):
+                    on_table(raw_ps[c, t], w1_w[a][:, P * t : P * (t + 1)], w1_s[a][:, P * t : P * (t + 1)], a, c)
+
+        raw_sb, f_planes, f_woven, f_w, f_s, e_ps = {}, {}, {}, {}, {}, {}
+        for c in range(2):
+            f_planes[c] = held("f_planes%d" % c, [P, PACK, HALF], BF16)
+            f_woven[c] = held("f_woven%d" % c, [P, PACK * HALF], BF16)
+            f_w[c] = held("f_w%d" % c, [P, HALF], U32)
+            f_s[c] = held("f_s%d" % c, [P, HALF], U8)
+        h = [rows.tile([P, S], F32, name="h%d" % t, tag="h") for t in range(PACK)]
+        page = [held("page%d" % t, [P, S], F32) for t in range(PACK)]
+        tops = held("tops", [P, 2 * PACK], F32)
+
+        def sine(c, t):
+            s = ring.tile([P, HALF], F32, name="s", tag="s")
+            nc.scalar.activation(out=s[:], in_=raw_ps[c, t][:], func=ACT.Sin, scale=third[:, t : t + 1])
+            sq = ring.tile([P, HALF], F32, name="sq", tag="sq")
+            nc.scalar.activation(out=sq[:], in_=s[:], func=ACT.Square, scale=root[:, t : t + 1])
+            return s, sq
+
+        def triple_angle(c, t, s, sq):
+            nc.vector.scalar_tensor_tensor(out=f_planes[c][:, t, :], in0=sq[:], scalar=triple[:, t : t + 1], in1=s[:],
+                                           op0=ALU.subtract, op1=ALU.mult)
+
+        def keep_raw(c, t, copy):
+            raw_sb[c, t] = held("raw%d%d" % (c, t), [P, HALF], F32)
+            copy(out=raw_sb[c, t][:], in_=raw_ps[c, t][:])
+
+        def second_product(c):
+            nc.vector.quantize_mx(out=f_w[c][:].bitcast(FP8X4), scales=f_s[c][:], in_=f_woven[c][:])
+            for t in range(PACK):
+                e_ps[c, t] = bank(PACK * c + t)
+                nc.tensor.matmul_mx(out=e_ps[c, t][:], lhsT=w2_w[:, 2 * P * t : 2 * P * (t + 1)].bitcast(FP4X4),
+                                    lhsT_scale=w2_s[:, P * t : P * (t + 1)], rhs=f_w[c][:].bitcast(FP8X4),
+                                    rhs_scale=f_s[c][:], start=True, stop=True)
+
+        def features(c, t):
+            cols = slice(HALF * c, HALF * (c + 1))
+            nc.vector.tensor_tensor(out=h[t][:, cols], in0=e_ps[c, t][:], in1=raw_sb[c, t][:], op=ALU.max)
+
+        def row_top(c, t):
+            cols = slice(HALF * c, HALF * (c + 1))
+            nc.vector.reduce_max(out=tops[:, 2 * t + c : 2 * t + c + 1], in_=h[t][:, cols], axis=AX.X)
+
+        def write_page(c, t):
+            cols = slice(HALF * c, HALF * (c + 1))
+            nc.scalar.activation(out=page[t][:, cols], in_=h[t][:, cols], func=ACT.Copy, scale=skip_t[:, t : t + 1])
+
+        for t in range(PACK):
+            s, sq = sine(0, t)
+            keep_raw(0, t, nc.vector.tensor_copy)
+            triple_angle(0, t, s, sq)
+        nc.vector.tensor_copy(out=woven(f_woven[0][:]), in_=weave(f_planes[0][:]))
+        second_product(0)
+        for t in range(PACK):
+            s, sq = sine(1, t)
+            triple_angle(1, t, s, sq)
+        for t in range(PACK):
+            features(0, t)
+        for t in range(PACK):
+            keep_raw(1, t, nc.scalar.copy)
+        nc.scalar.copy(out=woven(f_woven[1][:]), in_=weave(f_planes[1][:]))
+        second_product(1)
+        for t in range(PACK):
+            row_top(0, t)
+
+        w3_g = held("w3_g", [P, PACK * N], BF16)
+        nc.scalar.copy(out=woven(w3_g[:]), in_=weave(w3_in[:]))
+        for t in range(PACK):
+            write_page(0, t)
+        w3_w = held("w3_w", [P, N], U32)
+        w3_s = held("w3_s", [P, N], U8)
+        opening = held("opening", [P, PACK], F32)
+        nc.vector.scalar_tensor_tensor(out=opening[:], in0=slope_t[:], scalar=-1.0, in1=share_t[:], op0=ALU.mult, op1=ALU.mult)
+        bias = held("bias", [P, PACK], F32)
+
+        def look_bias(t):
+            nc.vector.tensor_scalar(out=bias[:, t : t + 1], in0=tops[:, 2 * t : 2 * t + 1], scalar1=tops[:, 2 * t + 1 : 2 * t + 2],
+                                    scalar2=opening[:, t : t + 1], op0=ALU.max, op1=ALU.mult)
+
+        features(1, 0)
+        for t in range(PACK):
+            if t + 1 < PACK:
+                features(1, t + 1)
+            row_top(1, t)
+            look_bias(t)
+        nc.vector.tensor_tensor(out=leaf_t[:], in0=leaf_t[:], in1=wgs_t[:], op=ALU.mult)
+        nc.vector.quantize_mx(out=w3_w[:].bitcast(FP8X4), scales=w3_s[:], in_=w3_g[:])
+
+        for t in range(PACK):
+            write_page(1, t)
+            look = rows.tile([P, L], F32, name="look", tag="look")
+            nc.scalar.activation(out=look[:], in_=h[t][:].indirect(p1[:]), func=ACT.Sigmoid,
+                                 bias=bias[:, t : t + 1], scale=slope_t[:, t : t + 1])
+            nc.vector.tensor_tensor(out=page[t][:].indirect(p2[:]), in0=look[:], in1=leaf_t[:, L * t : L * (t + 1)], op=ALU.mult)
+
+        g_planes = held("g_planes", [P, PACK, S], BF16)
+        bounded = []
+        for n in range(TILES):
+            tile = rows.tile([P, S], F32, name="bounded%d" % n, tag="h")
+            for c in range(2):
+                d_ps = bank(2 * n + c)
+                for a in range(PASSES):
+                    on_table(d_ps, w4_w[:, a, P * n : P * (n + 1)], w4_s[4 * a : P, P * n : P * (n + 1)], a, c)
+                nc.scalar.activation(out=tile[:, HALF * c : HALF * (c + 1)], in_=d_ps[:], func=ACT.Tanh)
+            bounded.append(tile)
+            nc.scalar.activation(out=g_planes[:, n, :], in_=page[n][:], func=ACT.Copy, scale=gain_t[:, n : n + 1])
+        last = PACK - 1
+        nc.vector.tensor_scalar(out=g_planes[:, last, :], in0=page[last][:], scalar1=gain_t[:, last : last + 1], scalar2=None, op0=ALU.mult)
+
+        g_w = held("g_w", [P, S], U32)
+        g_s = held("g_s", [P, S], U8)
+        y_ps = {}
+        for k in range(S // QUARTER):
+            c, cols = k // 2, slice(QUARTER * k, QUARTER * (k + 1))
+            g_woven = held("g_woven%d" % k, [P, PACK * QUARTER], BF16)
+            copy = nc.scalar.copy if k in (1, 2) else nc.vector.tensor_copy
+            copy(out=woven(g_woven[:]), in_=weave(g_planes[:, :, cols]))
+            nc.vector.quantize_mx(out=g_w[:, cols].bitcast(FP8X4), scales=g_s[:, cols], in_=g_woven[:])
+            for n in range(TILES):
+                if k % 2 == 0:
+                    y_ps[n, c] = bank((6 + TILES * c + n) % 8)
+                part = slice(QUARTER * (k % 2), QUARTER * (k % 2 + 1))
+                nc.tensor.matmul_mx(out=y_ps[n, c][:, part], lhsT=w3_w[:, P * n : P * (n + 1)].bitcast(FP8X4),
+                                    lhsT_scale=w3_s[:, P * n : P * (n + 1)], rhs=g_w[:, cols].bitcast(FP8X4),
+                                    rhs_scale=g_s[:, cols], start=True, stop=True)
+            if k % 2 == 1:
+                half = slice(HALF * c, HALF * (c + 1))
+                for n in range(TILES):
+                    result = ring.tile([P, HALF], F32, name="result", tag="result")
+                    nc.vector.tensor_tensor(out=result[:], in0=y_ps[n, c][:], in1=bounded[n][:, half], op=ALU.max)
+                    nc.sync.dma_start(out=out[P * n : P * (n + 1), half], in_=result[:])

@@ -23,6 +23,21 @@ HALF = 512
 PASSES = K // (P * PACK)
 TILES = N // P
 QUARTER = 256
+ZERO_SPLIT = 2560
+RAW0_V = 4
+E1_V = False
+E0_V = False
+PAGE_G = ()
+PAGE0_EARLY = 0
+E1_BANK = 0
+D_BANK = 4
+HB = 5
+M3_S = 0
+LW_G = False
+W3 = "S"
+W3_LATE = False
+N_S = (2, 3)
+LW_EARLY = True
 
 
 def weave(src):
@@ -59,43 +74,42 @@ def tile_list_onion_neck_features_kernel(
         idx = lists.tile([P, S // 16], U16, name="idx")
         p1 = lists.tile([P, L // 16], U16, name="p1")
         p2 = lists.tile([P, L // 16], U16, name="p2")
-        nc.sync.dma_start(idx[:], offs)
-
         tab_s = held("tab_s", [P, T], U8)
-        nc.vector.memset(tab_s[:].bitcast(I32), 0)
+        nc.gpsimd.memset(tab_s[:, :ZERO_SPLIT].bitcast(I32), 0)
+        nc.vector.memset(tab_s[:, ZERO_SPLIT:].bitcast(I32), 0)
         w2_s_in = held("w2_s_in", [P, H], U8)
-        nc.vector.memset(w2_s_in[:].bitcast(I32), 0)
+        nc.gpsimd.memset(w2_s_in[:].bitcast(I32), 0)
         w4_s = held("w4_s", [P, N], U8)
-        nc.vector.memset(w4_s[:].bitcast(I32), 0)
-        for q in range(4):
-            nc.gpsimd.dma_start(out=tab_s[32 * q : 32 * q + 8, :].bitcast(I32),
-                                in_=tab_scales[:, 4 * q : 4 * q + 4, :].bitcast(I32))
-        for q in range(4):
-            nc.gpsimd.dma_start(out=w2_s_in[32 * q : 32 * q + 4, :].bitcast(I32),
-                                in_=w2_scales[0, 4 * q : 4 * q + 4, :].bitcast(I32))
+        nc.gpsimd.memset(w4_s[:].bitcast(I32), 0)
 
-        swing_t = by_row("swing_t", swing, nc.scalar)
+        w1_in = [held("w1_in%d" % a, [P, PACK, H], F32) for a in range(PASSES)]
+        tab_w = [held("tab_w%d" % a, [P, T], U32) for a in range(PASSES)]
+
+        def load_w1(a):
+            nc.sync.dma_start(out=w1_in[a][:], in_=w1[512 * a : 512 * (a + 1), :].rearrange("(p j) c -> p j c", j=PACK))
+
+        nc.sync.dma_start(idx[:], offs)
+        load_w1(0)
+        swing_t = by_row("swing_t", swing, nc.sync)
         w2_in = held("w2_in", [P, 2 * H], U8)
-        nc.scalar.dma_start(out=w2_in[:].bitcast(I32), in_=w2_words[0].bitcast(I32))
-
-        w1_in = []
+        nc.sync.dma_start(out=w2_in[:].bitcast(I32), in_=w2_words[0].bitcast(I32))
+        for q in range(4):
+            nc.sync.dma_start(out=tab_s[32 * q : 32 * q + 8, :].bitcast(I32),
+                              in_=tab_scales[:, 4 * q : 4 * q + 4, :].bitcast(I32))
+        load_w1(1)
+        for q in range(4):
+            nc.sync.dma_start(out=w2_s_in[32 * q : 32 * q + 4, :].bitcast(I32),
+                              in_=w2_scales[0, 4 * q : 4 * q + 4, :].bitcast(I32))
         for a in range(PASSES):
-            tile = held("w1_in%d" % a, [P, PACK, H], F32)
-            nc.sync.dma_start(out=tile[:], in_=w1[512 * a : 512 * (a + 1), :].rearrange("(p j) c -> p j c", j=PACK))
-            w1_in.append(tile)
-        tab_w = []
-        for a in range(PASSES):
-            tile = held("tab_w%d" % a, [P, T], U32)
-            nc.sync.dma_start(out=tile[:].bitcast(I32), in_=tab_words[a].rearrange("p c i -> p (c i)").bitcast(I32))
-            tab_w.append(tile)
+            nc.sync.dma_start(out=tab_w[a][:].bitcast(I32), in_=tab_words[a].rearrange("p c i -> p (c i)").bitcast(I32))
         skip_t = by_row("skip_t", skip, nc.sync)
-        w3_in = held("w3_in", [P, PACK, N], F32)
-        nc.sync.dma_start(out=w3_in[:], in_=w3.rearrange("(p j) c -> p j c", j=PACK))
         leaf_t = held("leaf_t", [P, PACK * L], F32)
         nc.sync.dma_start(out=leaf_t[:], in_=leaf.rearrange("(p t) m -> p (t m)", t=PACK))
         wgs_t = held("wgs_t", [P, PACK * L], F32)
         for q in (0, 2, 1, 3):
             nc.sync.dma_start(out=wgs_t[32 * q : 32 * (q + 1), :], in_=wgs.rearrange("(p t) m -> p (t m)", t=PACK))
+        w3_in = held("w3_in", [P, PACK, N], F32)
+        nc.sync.dma_start(out=w3_in[:], in_=w3.rearrange("(p j) c -> p j c", j=PACK))
         w4_w = held("w4_w", [P, PASSES, N], U32)
         nc.sync.dma_start(out=w4_w[:].bitcast(I32), in_=w4_words.rearrange("a p c i -> p a (c i)").bitcast(I32))
         for q in range(4):
@@ -122,7 +136,7 @@ def tile_list_onion_neck_features_kernel(
                               in_=w2_in[:].rearrange("p (m t b) -> p m t b", t=PACK, b=2))
 
         w2_s = held("w2_s", [P, H], U8)
-        nc.gpsimd.tensor_copy(out=w2_s[:].rearrange("p (t m) -> p m t", t=PACK),
+        nc.vector.tensor_copy(out=w2_s[:].rearrange("p (t m) -> p m t", t=PACK),
                               in_=w2_s_in[:].rearrange("p (m t) -> p m t", t=PACK))
 
         w1_w, w1_s = [], []
@@ -163,8 +177,11 @@ def tile_list_onion_neck_features_kernel(
             f_woven[c] = held("f_woven%d" % c, [P, PACK * HALF], BF16)
             f_w[c] = held("f_w%d" % c, [P, HALF], U32)
             f_s[c] = held("f_s%d" % c, [P, HALF], U8)
-        h = [rows.tile([P, S], F32, name="h%d" % t, tag="h") for t in range(PACK)]
-        page = [held("page%d" % t, [P, S], F32) for t in range(PACK)]
+        h = [rows.tile([P, S], F32, name="h%d" % t, tag="h", bufs=HB) for t in range(PACK)]
+        page = [rows.tile([P, S], F32, name="page%d" % t, tag="h", bufs=HB) for t in range(PACK)]
+        if PAGE_G:
+            zero = held("zero", [P, 1], F32)
+            nc.gpsimd.memset(zero[:], 0.0)
         tops = held("tops", [P, 2 * PACK], F32)
 
         def sine(c, t):
@@ -185,7 +202,7 @@ def tile_list_onion_neck_features_kernel(
         def second_product(c):
             nc.vector.quantize_mx(out=f_w[c][:].bitcast(FP8X4), scales=f_s[c][:], in_=f_woven[c][:])
             for t in range(PACK):
-                e_ps[c, t] = bank(PACK * c + t)
+                e_ps[c, t] = bank(E1_BANK * c + t)
                 nc.tensor.matmul_mx(out=e_ps[c, t][:], lhsT=w2_w[:, 2 * P * t : 2 * P * (t + 1)].bitcast(FP4X4),
                                     lhsT_scale=w2_s[:, P * t : P * (t + 1)], rhs=f_w[c][:].bitcast(FP8X4),
                                     rhs_scale=f_s[c][:], start=True, stop=True)
@@ -199,40 +216,54 @@ def tile_list_onion_neck_features_kernel(
             nc.vector.reduce_max(out=tops[:, 2 * t + c : 2 * t + c + 1], in_=h[t][:, cols], axis=AX.X)
 
         def write_page(c, t):
-            cols = slice(HALF * c, HALF * (c + 1))
-            nc.scalar.activation(out=page[t][:, cols], in_=h[t][:, cols], func=ACT.Copy, scale=skip_t[:, t : t + 1])
+            cols = slice(HALF * c, HALF * (c + 1)) if c < 2 else slice(0, S)
+            if (c, t) in PAGE_G:
+                nc.gpsimd.tensor_scalar(out=page[t][:, cols], in0=h[t][:, cols], scalar1=skip_t[:, t : t + 1], scalar2=zero[:], op0=ALU.mult, op1=ALU.add)
+            else:
+                nc.scalar.activation(out=page[t][:, cols], in_=h[t][:, cols], func=ACT.Copy, scale=skip_t[:, t : t + 1])
+
+        def weigh():
+            for t in range(PACK):
+                cols = slice(L * t, L * (t + 1))
+                (nc.gpsimd if LW_G else nc.vector).tensor_tensor(out=leaf_t[:, cols], in0=leaf_t[:, cols], in1=wgs_t[:, cols], op=ALU.mult)
+
+        w3_g = held("w3_g", [P, PACK * N], BF16)
+        w3_w = held("w3_w", [P, N], U32)
+        w3_s = held("w3_s", [P, N], U8)
+        opening = held("opening", [P, PACK], F32)
+        bias = held("bias", [P, PACK], F32)
+
+        def look_bias(t):
+            nc.vector.tensor_scalar(out=bias[:, t : t + 1], in0=tops[:, 2 * t : 2 * t + 1], scalar1=tops[:, 2 * t + 1 : 2 * t + 2],
+                                    scalar2=opening[:, t : t + 1], op0=ALU.max, op1=ALU.mult)
+
+        def w3_weave():
+            (nc.gpsimd.tensor_copy if W3 == "G" else nc.scalar.copy if W3 == "S" else nc.vector.tensor_copy)(out=woven(w3_g[:]), in_=weave(w3_in[:]))
 
         for t in range(PACK):
             s, sq = sine(0, t)
-            keep_raw(0, t, nc.vector.tensor_copy)
+            keep_raw(0, t, nc.vector.tensor_copy if t < RAW0_V else nc.scalar.copy)
             triple_angle(0, t, s, sq)
-        nc.vector.tensor_copy(out=woven(f_woven[0][:]), in_=weave(f_planes[0][:]))
+        (nc.vector.tensor_copy if E0_V else nc.scalar.copy)(out=woven(f_woven[0][:]), in_=weave(f_planes[0][:]))
         second_product(0)
         for t in range(PACK):
             s, sq = sine(1, t)
             triple_angle(1, t, s, sq)
         for t in range(PACK):
             features(0, t)
+        (nc.vector.tensor_copy if E1_V else nc.scalar.copy)(out=woven(f_woven[1][:]), in_=weave(f_planes[1][:]))
         for t in range(PACK):
             keep_raw(1, t, nc.scalar.copy)
-        nc.scalar.copy(out=woven(f_woven[1][:]), in_=weave(f_planes[1][:]))
         second_product(1)
+        nc.vector.scalar_tensor_tensor(out=opening[:], in0=slope_t[:], scalar=-1.0, in1=share_t[:], op0=ALU.mult, op1=ALU.mult)
         for t in range(PACK):
             row_top(0, t)
-
-        w3_g = held("w3_g", [P, PACK * N], BF16)
-        nc.scalar.copy(out=woven(w3_g[:]), in_=weave(w3_in[:]))
-        for t in range(PACK):
+        if not W3_LATE:
+            w3_weave()
+        for t in range(PAGE0_EARLY):
             write_page(0, t)
-        w3_w = held("w3_w", [P, N], U32)
-        w3_s = held("w3_s", [P, N], U8)
-        opening = held("opening", [P, PACK], F32)
-        nc.vector.scalar_tensor_tensor(out=opening[:], in0=slope_t[:], scalar=-1.0, in1=share_t[:], op0=ALU.mult, op1=ALU.mult)
-        bias = held("bias", [P, PACK], F32)
-
-        def look_bias(t):
-            nc.vector.tensor_scalar(out=bias[:, t : t + 1], in0=tops[:, 2 * t : 2 * t + 1], scalar1=tops[:, 2 * t + 1 : 2 * t + 2],
-                                    scalar2=opening[:, t : t + 1], op0=ALU.max, op1=ALU.mult)
+        if LW_EARLY:
+            weigh()
 
         features(1, 0)
         for t in range(PACK):
@@ -240,49 +271,56 @@ def tile_list_onion_neck_features_kernel(
                 features(1, t + 1)
             row_top(1, t)
             look_bias(t)
-        nc.vector.tensor_tensor(out=leaf_t[:], in0=leaf_t[:], in1=wgs_t[:], op=ALU.mult)
-        nc.vector.quantize_mx(out=w3_w[:].bitcast(FP8X4), scales=w3_s[:], in_=w3_g[:])
+        if not LW_EARLY:
+            weigh()
 
         for t in range(PACK):
-            write_page(1, t)
             look = rows.tile([P, L], F32, name="look", tag="look")
             nc.scalar.activation(out=look[:], in_=h[t][:].indirect(p1[:]), func=ACT.Sigmoid,
                                  bias=bias[:, t : t + 1], scale=slope_t[:, t : t + 1])
+            write_page(1 if t < PAGE0_EARLY else 2, t)
             nc.vector.tensor_tensor(out=page[t][:].indirect(p2[:]), in0=look[:], in1=leaf_t[:, L * t : L * (t + 1)], op=ALU.mult)
+        if W3_LATE:
+            w3_weave()
+        nc.vector.quantize_mx(out=w3_w[:].bitcast(FP8X4), scales=w3_s[:], in_=w3_g[:])
 
         g_planes = held("g_planes", [P, PACK, S], BF16)
         bounded = []
         for n in range(TILES):
-            tile = rows.tile([P, S], F32, name="bounded%d" % n, tag="h")
+            tile = rows.tile([P, S], F32, name="bounded%d" % n, tag="h", bufs=HB)
             for c in range(2):
-                d_ps = bank(2 * n + c)
+                d_ps = bank((D_BANK + 2 * n + c) % 8)
                 for a in range(PASSES):
                     on_table(d_ps, w4_w[:, a, P * n : P * (n + 1)], w4_s[4 * a : P, P * n : P * (n + 1)], a, c)
                 nc.scalar.activation(out=tile[:, HALF * c : HALF * (c + 1)], in_=d_ps[:], func=ACT.Tanh)
             bounded.append(tile)
             nc.scalar.activation(out=g_planes[:, n, :], in_=page[n][:], func=ACT.Copy, scale=gain_t[:, n : n + 1])
         last = PACK - 1
-        nc.vector.tensor_scalar(out=g_planes[:, last, :], in0=page[last][:], scalar1=gain_t[:, last : last + 1], scalar2=None, op0=ALU.mult)
+        cut = S - M3_S
+        nc.vector.tensor_scalar(out=g_planes[:, last, :cut], in0=page[last][:, :cut], scalar1=gain_t[:, last : last + 1], scalar2=None, op0=ALU.mult)
+        if M3_S:
+            nc.scalar.activation(out=g_planes[:, last, cut:], in_=page[last][:, cut:], func=ACT.Copy, scale=gain_t[:, last : last + 1])
 
         g_w = held("g_w", [P, S], U32)
         g_s = held("g_s", [P, S], U8)
         y_ps = {}
-        for k in range(S // QUARTER):
+        quarters = S // QUARTER
+        for k in range(quarters):
             c, cols = k // 2, slice(QUARTER * k, QUARTER * (k + 1))
-            g_woven = held("g_woven%d" % k, [P, PACK * QUARTER], BF16)
-            copy = nc.scalar.copy if k in (1, 2) else nc.vector.tensor_copy
+            g_woven = keep.tile([P, PACK * QUARTER], BF16, name="g_woven%d" % k, tag="g_woven%d" % k, align_bytes=64)
+            copy = nc.scalar.copy if k in N_S else nc.vector.tensor_copy
             copy(out=woven(g_woven[:]), in_=weave(g_planes[:, :, cols]))
             nc.vector.quantize_mx(out=g_w[:, cols].bitcast(FP8X4), scales=g_s[:, cols], in_=g_woven[:])
             for n in range(TILES):
                 if k % 2 == 0:
-                    y_ps[n, c] = bank((6 + TILES * c + n) % 8)
+                    y_ps[n, c] = bank((D_BANK + 6 + TILES * c + n) % 8)
                 part = slice(QUARTER * (k % 2), QUARTER * (k % 2 + 1))
                 nc.tensor.matmul_mx(out=y_ps[n, c][:, part], lhsT=w3_w[:, P * n : P * (n + 1)].bitcast(FP8X4),
                                     lhsT_scale=w3_s[:, P * n : P * (n + 1)], rhs=g_w[:, cols].bitcast(FP8X4),
                                     rhs_scale=g_s[:, cols], start=True, stop=True)
-            if k % 2 == 1:
-                half = slice(HALF * c, HALF * (c + 1))
-                for n in range(TILES):
-                    result = ring.tile([P, HALF], F32, name="result", tag="result")
-                    nc.vector.tensor_tensor(out=result[:], in0=y_ps[n, c][:], in1=bounded[n][:, half], op=ALU.max)
-                    nc.sync.dma_start(out=out[P * n : P * (n + 1), half], in_=result[:])
+        for c in range(2):
+            half = slice(HALF * c, HALF * (c + 1))
+            result = keep.tile([P, TILES, HALF], F32, name="result%d" % c, tag="g_woven%d" % (quarters - 1 - c), align_bytes=64)
+            for n in range(TILES):
+                nc.vector.tensor_tensor(out=result[:, n, :], in0=y_ps[n, c][:], in1=bounded[n][:, half], op=ALU.max)
+                nc.sync.dma_start(out=out[P * n : P * (n + 1), half], in_=result[:, n, :])

@@ -23,21 +23,18 @@ HALF = 512
 PASSES = K // (P * PACK)
 TILES = N // P
 QUARTER = 256
-ZERO_SPLIT = 2560
-RAW0_V = 4
-E1_V = False
-E0_V = False
-PAGE_G = ()
-PAGE0_EARLY = 0
-E1_BANK = 0
-D_BANK = 4
+RAW_V = ((0, 0), (0, 1))
+SQ_V = ((0, 0), (1, 0))
 HB = 5
-M3_S = 0
-LW_G = False
-W3 = "S"
-W3_LATE = False
+M3_S = 512
 N_S = (2, 3)
-LW_EARLY = True
+SCALE_G = True
+W2S_G = True
+LW_G = True
+F_PARTS = (1, 2)
+W3_AFTER = 0
+B_OWN = 0
+WEAVE_S = ((1, 1),)
 
 
 def weave(src):
@@ -60,27 +57,26 @@ def tile_list_onion_neck_features_kernel(
         rows = ctx.enter_context(tc.tile_pool(name="rows", bufs=4))
         psum = ctx.enter_context(tc.psum_pool(name="psum", bufs=1))
 
-        def held(name, shape, dtype):
-            return keep.tile(shape, dtype, name=name, align_bytes=64)
+        def held(name, shape, dtype, tag=None):
+            return keep.tile(shape, dtype, name=name, tag=tag or name, align_bytes=64)
 
         def bank(b):
             return psum.tile([P, HALF], F32, name="bank%d" % b, tag="bank%d" % b)
 
-        def by_row(name, vec, queue):
+        def by_row(name, vec):
             tile = held(name, [P, PACK], F32)
-            queue.dma_start(out=tile[:], in_=vec.rearrange("(p t) -> p t", t=PACK))
+            nc.sync.dma_start(out=tile[:], in_=vec.rearrange("(p t) -> p t", t=PACK))
             return tile
 
         idx = lists.tile([P, S // 16], U16, name="idx")
         p1 = lists.tile([P, L // 16], U16, name="p1")
         p2 = lists.tile([P, L // 16], U16, name="p2")
         tab_s = held("tab_s", [P, T], U8)
-        nc.gpsimd.memset(tab_s[:, :ZERO_SPLIT].bitcast(I32), 0)
-        nc.vector.memset(tab_s[:, ZERO_SPLIT:].bitcast(I32), 0)
+        nc.vector.memset(tab_s[:].bitcast(I32), 0)
         w2_s_in = held("w2_s_in", [P, H], U8)
-        nc.gpsimd.memset(w2_s_in[:].bitcast(I32), 0)
+        nc.vector.memset(w2_s_in[:].bitcast(I32), 0)
         w4_s = held("w4_s", [P, N], U8)
-        nc.gpsimd.memset(w4_s[:].bitcast(I32), 0)
+        nc.vector.memset(w4_s[:].bitcast(I32), 0)
 
         w1_in = [held("w1_in%d" % a, [P, PACK, H], F32) for a in range(PASSES)]
         tab_w = [held("tab_w%d" % a, [P, T], U32) for a in range(PASSES)]
@@ -88,26 +84,40 @@ def tile_list_onion_neck_features_kernel(
         def load_w1(a):
             nc.sync.dma_start(out=w1_in[a][:], in_=w1[512 * a : 512 * (a + 1), :].rearrange("(p j) c -> p j c", j=PACK))
 
+        def load_tab_s(queue):
+            for q in range(4):
+                queue.dma_start(out=tab_s[32 * q : 32 * q + 8, :].bitcast(I32),
+                                in_=tab_scales[:, 4 * q : 4 * q + 4, :].bitcast(I32))
+
+        def load_w2_s(queue):
+            for q in range(4):
+                queue.dma_start(out=w2_s_in[32 * q : 32 * q + 4, :].bitcast(I32),
+                                in_=w2_scales[0, 4 * q : 4 * q + 4, :].bitcast(I32))
+
         nc.sync.dma_start(idx[:], offs)
+        swing_t = by_row("swing_t", swing)
         load_w1(0)
-        swing_t = by_row("swing_t", swing, nc.sync)
+        load_tab_s(nc.gpsimd if SCALE_G else nc.sync)
         w2_in = held("w2_in", [P, 2 * H], U8)
-        nc.sync.dma_start(out=w2_in[:].bitcast(I32), in_=w2_words[0].bitcast(I32))
-        for q in range(4):
-            nc.sync.dma_start(out=tab_s[32 * q : 32 * q + 8, :].bitcast(I32),
-                              in_=tab_scales[:, 4 * q : 4 * q + 4, :].bitcast(I32))
+        if W2S_G:
+            nc.sync.dma_start(out=w2_in[:].bitcast(I32), in_=w2_words[0].bitcast(I32))
+            load_w2_s(nc.gpsimd)
         load_w1(1)
-        for q in range(4):
-            nc.sync.dma_start(out=w2_s_in[32 * q : 32 * q + 4, :].bitcast(I32),
-                              in_=w2_scales[0, 4 * q : 4 * q + 4, :].bitcast(I32))
         for a in range(PASSES):
             nc.sync.dma_start(out=tab_w[a][:].bitcast(I32), in_=tab_words[a].rearrange("p c i -> p (c i)").bitcast(I32))
-        skip_t = by_row("skip_t", skip, nc.sync)
+        if not W2S_G:
+            nc.sync.dma_start(out=w2_in[:].bitcast(I32), in_=w2_words[0].bitcast(I32))
+            load_w2_s(nc.sync)
+        slope_t = by_row("slope_t", slope)
+        share_t = by_row("share_t", share)
         leaf_t = held("leaf_t", [P, PACK * L], F32)
         nc.sync.dma_start(out=leaf_t[:], in_=leaf.rearrange("(p t) m -> p (t m)", t=PACK))
         wgs_t = held("wgs_t", [P, PACK * L], F32)
         for q in (0, 2, 1, 3):
             nc.sync.dma_start(out=wgs_t[32 * q : 32 * (q + 1), :], in_=wgs.rearrange("(p t) m -> p (t m)", t=PACK))
+        skip_t = by_row("skip_t", skip)
+        nc.sync.dma_start(p1[:], pos1)
+        nc.sync.dma_start(p2[:], pos2)
         w3_in = held("w3_in", [P, PACK, N], F32)
         nc.sync.dma_start(out=w3_in[:], in_=w3.rearrange("(p j) c -> p j c", j=PACK))
         w4_w = held("w4_w", [P, PASSES, N], U32)
@@ -115,11 +125,7 @@ def tile_list_onion_neck_features_kernel(
         for q in range(4):
             nc.sync.dma_start(out=w4_s[32 * q : 32 * q + 8, :].bitcast(I32),
                               in_=w4_scales[:, 4 * q : 4 * q + 4, :].bitcast(I32))
-        nc.sync.dma_start(p1[:], pos1)
-        nc.sync.dma_start(p2[:], pos2)
-        slope_t = by_row("slope_t", slope, nc.sync)
-        share_t = by_row("share_t", share, nc.sync)
-        gain_t = by_row("gain_t", gain, nc.sync)
+        gain_t = by_row("gain_t", gain)
 
         third = held("third", [P, PACK], F32)
         nc.vector.tensor_scalar(out=third[:], in0=swing_t[:], scalar1=0.0, scalar2=None, op0=ALU.is_ge)
@@ -130,14 +136,9 @@ def tile_list_onion_neck_features_kernel(
         nc.scalar.activation(out=root[:], in_=size[:], func=ACT.Sqrt, scale=4.0)
         triple = held("triple", [P, PACK], F32)
         nc.vector.tensor_scalar(out=triple[:], in0=size[:], scalar1=3.0, scalar2=None, op0=ALU.mult)
-
-        w2_w = held("w2_w", [P, 2 * H], U8)
-        nc.vector.tensor_copy(out=w2_w[:].rearrange("p (t m b) -> p m t b", t=PACK, b=2),
-                              in_=w2_in[:].rearrange("p (m t b) -> p m t b", t=PACK, b=2))
-
-        w2_s = held("w2_s", [P, H], U8)
-        nc.vector.tensor_copy(out=w2_s[:].rearrange("p (t m) -> p m t", t=PACK),
-                              in_=w2_s_in[:].rearrange("p (m t) -> p m t", t=PACK))
+        if SQ_V:
+            four = held("four", [P, PACK], F32)
+            nc.vector.tensor_scalar(out=four[:], in0=size[:], scalar1=4.0, scalar2=None, op0=ALU.mult)
 
         w1_w, w1_s = [], []
         for a in range(PASSES):
@@ -171,6 +172,13 @@ def tile_list_onion_neck_features_kernel(
                 for t in range(PACK):
                     on_table(raw_ps[c, t], w1_w[a][:, P * t : P * (t + 1)], w1_s[a][:, P * t : P * (t + 1)], a, c)
 
+        w2_w = held("w2_w", [P, 2 * H], U8)
+        nc.vector.tensor_copy(out=w2_w[:].rearrange("p (t m b) -> p m t b", t=PACK, b=2),
+                              in_=w2_in[:].rearrange("p (m t b) -> p m t b", t=PACK, b=2))
+        w2_s = held("w2_s", [P, H], U8)
+        nc.vector.tensor_copy(out=w2_s[:].rearrange("p (t m) -> p m t", t=PACK),
+                              in_=w2_s_in[:].rearrange("p (m t) -> p m t", t=PACK))
+
         raw_sb, f_planes, f_woven, f_w, f_s, e_ps = {}, {}, {}, {}, {}, {}
         for c in range(2):
             f_planes[c] = held("f_planes%d" % c, [P, PACK, HALF], BF16)
@@ -179,19 +187,18 @@ def tile_list_onion_neck_features_kernel(
             f_s[c] = held("f_s%d" % c, [P, HALF], U8)
         h = [rows.tile([P, S], F32, name="h%d" % t, tag="h", bufs=HB) for t in range(PACK)]
         page = [rows.tile([P, S], F32, name="page%d" % t, tag="h", bufs=HB) for t in range(PACK)]
-        if PAGE_G:
-            zero = held("zero", [P, 1], F32)
-            nc.gpsimd.memset(zero[:], 0.0)
-        tops = held("tops", [P, 2 * PACK], F32)
+        top = held("top", [P, PACK], F32)
+        opening = held("opening", [P, PACK], F32)
+        bias = held("bias", [P, PACK], F32)
 
         def sine(c, t):
             s = ring.tile([P, HALF], F32, name="s", tag="s")
             nc.scalar.activation(out=s[:], in_=raw_ps[c, t][:], func=ACT.Sin, scale=third[:, t : t + 1])
             sq = ring.tile([P, HALF], F32, name="sq", tag="sq")
-            nc.scalar.activation(out=sq[:], in_=s[:], func=ACT.Square, scale=root[:, t : t + 1])
-            return s, sq
-
-        def triple_angle(c, t, s, sq):
+            if (c, t) in SQ_V:
+                nc.vector.scalar_tensor_tensor(out=sq[:], in0=s[:], scalar=four[:, t : t + 1], in1=s[:], op0=ALU.mult, op1=ALU.mult)
+            else:
+                nc.scalar.activation(out=sq[:], in_=s[:], func=ACT.Square, scale=root[:, t : t + 1])
             nc.vector.scalar_tensor_tensor(out=f_planes[c][:, t, :], in0=sq[:], scalar=triple[:, t : t + 1], in1=s[:],
                                            op0=ALU.subtract, op1=ALU.mult)
 
@@ -199,97 +206,69 @@ def tile_list_onion_neck_features_kernel(
             raw_sb[c, t] = held("raw%d%d" % (c, t), [P, HALF], F32)
             copy(out=raw_sb[c, t][:], in_=raw_ps[c, t][:])
 
-        def second_product(c):
-            nc.vector.quantize_mx(out=f_w[c][:].bitcast(FP8X4), scales=f_s[c][:], in_=f_woven[c][:])
-            for t in range(PACK):
-                e_ps[c, t] = bank(E1_BANK * c + t)
-                nc.tensor.matmul_mx(out=e_ps[c, t][:], lhsT=w2_w[:, 2 * P * t : 2 * P * (t + 1)].bitcast(FP4X4),
-                                    lhsT_scale=w2_s[:, P * t : P * (t + 1)], rhs=f_w[c][:].bitcast(FP8X4),
-                                    rhs_scale=f_s[c][:], start=True, stop=True)
+        def quantise_f(c):
+            width = HALF // F_PARTS[c]
+            for i in range(F_PARTS[c]):
+                (nc.scalar.copy if (c, i) in WEAVE_S else nc.vector.tensor_copy)(out=woven(f_woven[c][:, PACK * width * i : PACK * width * (i + 1)]),
+                                      in_=weave(f_planes[c][:, :, width * i : width * (i + 1)]))
+            for i in range(F_PARTS[c]):
+                cols = slice(width * i, width * (i + 1))
+                nc.vector.quantize_mx(out=f_w[c][:, cols].bitcast(FP8X4), scales=f_s[c][:, cols],
+                                      in_=f_woven[c][:, PACK * width * i : PACK * width * (i + 1)])
+
+        def second_product(c, t):
+            e_ps[c, t] = bank(PACK * c + t)
+            nc.tensor.matmul_mx(out=e_ps[c, t][:], lhsT=w2_w[:, 2 * P * t : 2 * P * (t + 1)].bitcast(FP4X4),
+                                lhsT_scale=w2_s[:, P * t : P * (t + 1)], rhs=f_w[c][:].bitcast(FP8X4),
+                                rhs_scale=f_s[c][:], start=True, stop=True)
 
         def features(c, t):
             cols = slice(HALF * c, HALF * (c + 1))
             nc.vector.tensor_tensor(out=h[t][:, cols], in0=e_ps[c, t][:], in1=raw_sb[c, t][:], op=ALU.max)
 
-        def row_top(c, t):
-            cols = slice(HALF * c, HALF * (c + 1))
-            nc.vector.reduce_max(out=tops[:, 2 * t + c : 2 * t + c + 1], in_=h[t][:, cols], axis=AX.X)
-
-        def write_page(c, t):
-            cols = slice(HALF * c, HALF * (c + 1)) if c < 2 else slice(0, S)
-            if (c, t) in PAGE_G:
-                nc.gpsimd.tensor_scalar(out=page[t][:, cols], in0=h[t][:, cols], scalar1=skip_t[:, t : t + 1], scalar2=zero[:], op0=ALU.mult, op1=ALU.add)
-            else:
-                nc.scalar.activation(out=page[t][:, cols], in_=h[t][:, cols], func=ACT.Copy, scale=skip_t[:, t : t + 1])
-
-        def weigh():
+        for c in range(2):
             for t in range(PACK):
-                cols = slice(L * t, L * (t + 1))
-                (nc.gpsimd if LW_G else nc.vector).tensor_tensor(out=leaf_t[:, cols], in0=leaf_t[:, cols], in1=wgs_t[:, cols], op=ALU.mult)
-
-        w3_g = held("w3_g", [P, PACK * N], BF16)
-        w3_w = held("w3_w", [P, N], U32)
-        w3_s = held("w3_s", [P, N], U8)
-        opening = held("opening", [P, PACK], F32)
-        bias = held("bias", [P, PACK], F32)
-
-        def look_bias(t):
-            nc.vector.tensor_scalar(out=bias[:, t : t + 1], in0=tops[:, 2 * t : 2 * t + 1], scalar1=tops[:, 2 * t + 1 : 2 * t + 2],
-                                    scalar2=opening[:, t : t + 1], op0=ALU.max, op1=ALU.mult)
-
-        def w3_weave():
-            (nc.gpsimd.tensor_copy if W3 == "G" else nc.scalar.copy if W3 == "S" else nc.vector.tensor_copy)(out=woven(w3_g[:]), in_=weave(w3_in[:]))
-
-        for t in range(PACK):
-            s, sq = sine(0, t)
-            keep_raw(0, t, nc.vector.tensor_copy if t < RAW0_V else nc.scalar.copy)
-            triple_angle(0, t, s, sq)
-        (nc.vector.tensor_copy if E0_V else nc.scalar.copy)(out=woven(f_woven[0][:]), in_=weave(f_planes[0][:]))
-        second_product(0)
-        for t in range(PACK):
-            s, sq = sine(1, t)
-            triple_angle(1, t, s, sq)
-        for t in range(PACK):
-            features(0, t)
-        (nc.vector.tensor_copy if E1_V else nc.scalar.copy)(out=woven(f_woven[1][:]), in_=weave(f_planes[1][:]))
-        for t in range(PACK):
-            keep_raw(1, t, nc.scalar.copy)
-        second_product(1)
+                sine(c, t)
+                if (c, t) in RAW_V:
+                    keep_raw(c, t, nc.vector.tensor_copy)
+            quantise_f(c)
         nc.vector.scalar_tensor_tensor(out=opening[:], in0=slope_t[:], scalar=-1.0, in1=share_t[:], op0=ALU.mult, op1=ALU.mult)
         for t in range(PACK):
-            row_top(0, t)
-        if not W3_LATE:
-            w3_weave()
-        for t in range(PAGE0_EARLY):
-            write_page(0, t)
-        if LW_EARLY:
-            weigh()
-
-        features(1, 0)
+            for c in range(2):
+                if (c, t) not in RAW_V:
+                    keep_raw(c, t, nc.scalar.copy)
+        weight = held("weight", [P, PACK * L], F32, tag="f_woven1")
         for t in range(PACK):
-            if t + 1 < PACK:
-                features(1, t + 1)
-            row_top(1, t)
-            look_bias(t)
-        if not LW_EARLY:
-            weigh()
-
+            cols = slice(L * t, L * (t + 1))
+            (nc.gpsimd if LW_G else nc.vector).tensor_tensor(out=weight[:, cols], in0=leaf_t[:, cols], in1=wgs_t[:, cols], op=ALU.mult)
         for t in range(PACK):
-            look = rows.tile([P, L], F32, name="look", tag="look")
+            for c in range(2):
+                second_product(c, t)
+                features(c, t)
+            nc.vector.reduce_max(out=top[:, t : t + 1], in_=h[t][:], axis=AX.X)
+
+        w3_g = held("w3_g", [P, PACK * N], BF16)
+        w3_s = held("w3_s", [P, N], U8)
+        for t in range(PACK):
+            nc.scalar.activation(out=bias[:, t : t + 1], in_=top[:, t : t + 1], func=ACT.Copy, scale=opening[:, t : t + 1])
+            look = keep.tile([P, L], F32, name="look%d" % t, tag="look%d" % t, align_bytes=64)
             nc.scalar.activation(out=look[:], in_=h[t][:].indirect(p1[:]), func=ACT.Sigmoid,
                                  bias=bias[:, t : t + 1], scale=slope_t[:, t : t + 1])
-            write_page(1 if t < PAGE0_EARLY else 2, t)
-            nc.vector.tensor_tensor(out=page[t][:].indirect(p2[:]), in0=look[:], in1=leaf_t[:, L * t : L * (t + 1)], op=ALU.mult)
-        if W3_LATE:
-            w3_weave()
+            nc.scalar.activation(out=page[t][:], in_=h[t][:], func=ACT.Copy, scale=skip_t[:, t : t + 1])
+            nc.vector.tensor_tensor(out=page[t][:].indirect(p2[:]), in0=look[:], in1=weight[:, L * t : L * (t + 1)], op=ALU.mult)
+        nc.scalar.copy(out=woven(w3_g[:]), in_=weave(w3_in[:]))
+        w3_w = held("w3_w", [P, N], U32, tag="look%d" % W3_AFTER)
         nc.vector.quantize_mx(out=w3_w[:].bitcast(FP8X4), scales=w3_s[:], in_=w3_g[:])
 
         g_planes = held("g_planes", [P, PACK, S], BF16)
         bounded = []
         for n in range(TILES):
-            tile = rows.tile([P, S], F32, name="bounded%d" % n, tag="h", bufs=HB)
+            if n < B_OWN:
+                tile = held("bounded%d" % n, [P, S], F32)
+            else:
+                tile = rows.tile([P, S], F32, name="bounded%d" % n, tag="h", bufs=HB)
             for c in range(2):
-                d_ps = bank((D_BANK + 2 * n + c) % 8)
+                d_ps = bank(PACK * c + n)
                 for a in range(PASSES):
                     on_table(d_ps, w4_w[:, a, P * n : P * (n + 1)], w4_s[4 * a : P, P * n : P * (n + 1)], a, c)
                 nc.scalar.activation(out=tile[:, HALF * c : HALF * (c + 1)], in_=d_ps[:], func=ACT.Tanh)
@@ -313,7 +292,7 @@ def tile_list_onion_neck_features_kernel(
             nc.vector.quantize_mx(out=g_w[:, cols].bitcast(FP8X4), scales=g_s[:, cols], in_=g_woven[:])
             for n in range(TILES):
                 if k % 2 == 0:
-                    y_ps[n, c] = bank((D_BANK + 6 + TILES * c + n) % 8)
+                    y_ps[n, c] = bank((3, 7, 0, 4, 1, 5)[TILES * c + n])
                 part = slice(QUARTER * (k % 2), QUARTER * (k % 2 + 1))
                 nc.tensor.matmul_mx(out=y_ps[n, c][:, part], lhsT=w3_w[:, P * n : P * (n + 1)].bitcast(FP8X4),
                                     lhsT_scale=w3_s[:, P * n : P * (n + 1)], rhs=g_w[:, cols].bitcast(FP8X4),

@@ -29,11 +29,10 @@ HB = 5
 M3_S = 512
 N_S = (2, 3)
 SCALE_G = True
-W2S_G = True
-LW_G = True
+LW_G = False
 F_PARTS = (1, 2)
-W3_AFTER = 0
-B_OWN = 0
+B_OWN = 3
+RES = (3, 2)
 WEAVE_S = ((1, 1),)
 
 
@@ -53,7 +52,7 @@ def tile_list_onion_neck_features_kernel(
     with ExitStack() as ctx:
         lists = ctx.enter_context(tc.tile_pool(name="lists", bufs=1))
         keep = ctx.enter_context(tc.tile_pool(name="keep", bufs=1))
-        ring = ctx.enter_context(tc.tile_pool(name="ring", bufs=3))
+        ring = ctx.enter_context(tc.tile_pool(name="ring", bufs=4))
         rows = ctx.enter_context(tc.tile_pool(name="rows", bufs=4))
         psum = ctx.enter_context(tc.psum_pool(name="psum", bufs=1))
 
@@ -99,15 +98,11 @@ def tile_list_onion_neck_features_kernel(
         load_w1(0)
         load_tab_s(nc.gpsimd if SCALE_G else nc.sync)
         w2_in = held("w2_in", [P, 2 * H], U8)
-        if W2S_G:
-            nc.sync.dma_start(out=w2_in[:].bitcast(I32), in_=w2_words[0].bitcast(I32))
-            load_w2_s(nc.gpsimd)
+        nc.sync.dma_start(out=w2_in[:].bitcast(I32), in_=w2_words[0].bitcast(I32))
         load_w1(1)
         for a in range(PASSES):
             nc.sync.dma_start(out=tab_w[a][:].bitcast(I32), in_=tab_words[a].rearrange("p c i -> p (c i)").bitcast(I32))
-        if not W2S_G:
-            nc.sync.dma_start(out=w2_in[:].bitcast(I32), in_=w2_words[0].bitcast(I32))
-            load_w2_s(nc.sync)
+        load_w2_s(nc.sync)
         slope_t = by_row("slope_t", slope)
         share_t = by_row("share_t", share)
         leaf_t = held("leaf_t", [P, PACK * L], F32)
@@ -143,8 +138,8 @@ def tile_list_onion_neck_features_kernel(
         w1_w, w1_s = [], []
         for a in range(PASSES):
             grouped = held("w1_g%d" % a, [P, PACK * H], BF16)
-            nc.scalar.copy(out=grouped[:].rearrange("p (t m j) -> p m j t", t=PACK, j=PACK),
-                           in_=w1_in[a][:].rearrange("p j (m t) -> p m j t", t=PACK))
+            nc.scalar.copy(out=grouped[:].rearrange("p (t m j) -> p t m j", t=PACK, j=PACK),
+                           in_=w1_in[a][:].rearrange("p j (m t) -> p t m j", t=PACK))
             words = held("w1_w%d" % a, [P, H], U32)
             scales = held("w1_s%d" % a, [P, H], U8)
             nc.vector.quantize_mx(out=words[:].bitcast(FP8X4), scales=scales[:], in_=grouped[:])
@@ -173,11 +168,11 @@ def tile_list_onion_neck_features_kernel(
                     on_table(raw_ps[c, t], w1_w[a][:, P * t : P * (t + 1)], w1_s[a][:, P * t : P * (t + 1)], a, c)
 
         w2_w = held("w2_w", [P, 2 * H], U8)
-        nc.vector.tensor_copy(out=w2_w[:].rearrange("p (t m b) -> p m t b", t=PACK, b=2),
-                              in_=w2_in[:].rearrange("p (m t b) -> p m t b", t=PACK, b=2))
+        nc.vector.tensor_copy(out=w2_w[:].rearrange("p (t m b) -> p t m b", t=PACK, b=2),
+                              in_=w2_in[:].rearrange("p (m t b) -> p t m b", t=PACK, b=2))
         w2_s = held("w2_s", [P, H], U8)
-        nc.vector.tensor_copy(out=w2_s[:].rearrange("p (t m) -> p m t", t=PACK),
-                              in_=w2_s_in[:].rearrange("p (m t) -> p m t", t=PACK))
+        nc.vector.tensor_copy(out=w2_s[:].rearrange("p (t m) -> p t m", t=PACK),
+                              in_=w2_s_in[:].rearrange("p (m t) -> p t m", t=PACK))
 
         raw_sb, f_planes, f_woven, f_w, f_s, e_ps = {}, {}, {}, {}, {}, {}
         for c in range(2):
@@ -237,15 +232,15 @@ def tile_list_onion_neck_features_kernel(
             for c in range(2):
                 if (c, t) not in RAW_V:
                     keep_raw(c, t, nc.scalar.copy)
-        weight = held("weight", [P, PACK * L], F32, tag="f_woven1")
-        for t in range(PACK):
-            cols = slice(L * t, L * (t + 1))
-            (nc.gpsimd if LW_G else nc.vector).tensor_tensor(out=weight[:, cols], in0=leaf_t[:, cols], in1=wgs_t[:, cols], op=ALU.mult)
         for t in range(PACK):
             for c in range(2):
                 second_product(c, t)
                 features(c, t)
             nc.vector.reduce_max(out=top[:, t : t + 1], in_=h[t][:], axis=AX.X)
+        weight = held("weight", [P, PACK * L], F32, tag="f_woven1")
+        for t in range(PACK):
+            cols = slice(L * t, L * (t + 1))
+            (nc.gpsimd if LW_G else nc.vector).tensor_tensor(out=weight[:, cols], in0=leaf_t[:, cols], in1=wgs_t[:, cols], op=ALU.mult)
 
         w3_g = held("w3_g", [P, PACK * N], BF16)
         w3_s = held("w3_s", [P, N], U8)
@@ -257,7 +252,7 @@ def tile_list_onion_neck_features_kernel(
             nc.scalar.activation(out=page[t][:], in_=h[t][:], func=ACT.Copy, scale=skip_t[:, t : t + 1])
             nc.vector.tensor_tensor(out=page[t][:].indirect(p2[:]), in0=look[:], in1=weight[:, L * t : L * (t + 1)], op=ALU.mult)
         nc.scalar.copy(out=woven(w3_g[:]), in_=weave(w3_in[:]))
-        w3_w = held("w3_w", [P, N], U32, tag="look%d" % W3_AFTER)
+        w3_w = held("w3_w", [P, N], U32)
         nc.vector.quantize_mx(out=w3_w[:].bitcast(FP8X4), scales=w3_s[:], in_=w3_g[:])
 
         g_planes = held("g_planes", [P, PACK, S], BF16)
@@ -299,7 +294,7 @@ def tile_list_onion_neck_features_kernel(
                                     rhs_scale=g_s[:, cols], start=True, stop=True)
         for c in range(2):
             half = slice(HALF * c, HALF * (c + 1))
-            result = keep.tile([P, TILES, HALF], F32, name="result%d" % c, tag="g_woven%d" % (quarters - 1 - c), align_bytes=64)
+            result = keep.tile([P, TILES, HALF], F32, name="result%d" % c, tag="g_woven%d" % RES[c], align_bytes=64)
             for n in range(TILES):
                 nc.vector.tensor_tensor(out=result[:, n, :], in0=y_ps[n, c][:], in1=bounded[n][:, half], op=ALU.max)
                 nc.sync.dma_start(out=out[P * n : P * (n + 1), half], in_=result[:, n, :])

@@ -20,20 +20,13 @@ AX = mybir.AxisListType
 P = 128
 PACK = 4
 HALF = 512
+QUARTER = 256
 PASSES = K // (P * PACK)
 TILES = N // P
-QUARTER = 256
-RAW_V = ((0, 0), (0, 1))
-SQ_V = ((0, 0), (1, 0))
-HB = 5
-M3_S = 512
-N_S = (2, 3)
-SCALE_G = True
-LW_G = False
-F_PARTS = (1, 2)
-B_OWN = 3
-RES = (3, 2)
-WEAVE_S = ((1, 1),)
+QUADRANTS = 4
+SINE_BUFS = 4
+ROW_BUFS = PACK + 1
+VECTOR_SQUARES = 3
 
 
 def weave(src):
@@ -52,8 +45,8 @@ def tile_list_onion_neck_features_kernel(
     with ExitStack() as ctx:
         lists = ctx.enter_context(tc.tile_pool(name="lists", bufs=1))
         keep = ctx.enter_context(tc.tile_pool(name="keep", bufs=1))
-        ring = ctx.enter_context(tc.tile_pool(name="ring", bufs=4))
-        rows = ctx.enter_context(tc.tile_pool(name="rows", bufs=4))
+        ring = ctx.enter_context(tc.tile_pool(name="ring", bufs=SINE_BUFS))
+        rows = ctx.enter_context(tc.tile_pool(name="rows", bufs=ROW_BUFS))
         psum = ctx.enter_context(tc.psum_pool(name="psum", bufs=1))
 
         def held(name, shape, dtype, tag=None):
@@ -83,26 +76,20 @@ def tile_list_onion_neck_features_kernel(
         def load_w1(a):
             nc.sync.dma_start(out=w1_in[a][:], in_=w1[512 * a : 512 * (a + 1), :].rearrange("(p j) c -> p j c", j=PACK))
 
-        def load_tab_s(queue):
-            for q in range(4):
-                queue.dma_start(out=tab_s[32 * q : 32 * q + 8, :].bitcast(I32),
-                                in_=tab_scales[:, 4 * q : 4 * q + 4, :].bitcast(I32))
-
-        def load_w2_s(queue):
-            for q in range(4):
-                queue.dma_start(out=w2_s_in[32 * q : 32 * q + 4, :].bitcast(I32),
-                                in_=w2_scales[0, 4 * q : 4 * q + 4, :].bitcast(I32))
-
         nc.sync.dma_start(idx[:], offs)
         swing_t = by_row("swing_t", swing)
         load_w1(0)
-        load_tab_s(nc.gpsimd if SCALE_G else nc.sync)
+        for q in range(QUADRANTS):
+            nc.gpsimd.dma_start(out=tab_s[32 * q : 32 * q + 8, :].bitcast(I32),
+                                in_=tab_scales[:, 4 * q : 4 * q + 4, :].bitcast(I32))
         w2_in = held("w2_in", [P, 2 * H], U8)
         nc.sync.dma_start(out=w2_in[:].bitcast(I32), in_=w2_words[0].bitcast(I32))
         load_w1(1)
         for a in range(PASSES):
             nc.sync.dma_start(out=tab_w[a][:].bitcast(I32), in_=tab_words[a].rearrange("p c i -> p (c i)").bitcast(I32))
-        load_w2_s(nc.sync)
+        for q in range(QUADRANTS):
+            nc.sync.dma_start(out=w2_s_in[32 * q : 32 * q + 4, :].bitcast(I32),
+                              in_=w2_scales[0, 4 * q : 4 * q + 4, :].bitcast(I32))
         slope_t = by_row("slope_t", slope)
         share_t = by_row("share_t", share)
         leaf_t = held("leaf_t", [P, PACK * L], F32)
@@ -117,7 +104,7 @@ def tile_list_onion_neck_features_kernel(
         nc.sync.dma_start(out=w3_in[:], in_=w3.rearrange("(p j) c -> p j c", j=PACK))
         w4_w = held("w4_w", [P, PASSES, N], U32)
         nc.sync.dma_start(out=w4_w[:].bitcast(I32), in_=w4_words.rearrange("a p c i -> p a (c i)").bitcast(I32))
-        for q in range(4):
+        for q in range(QUADRANTS):
             nc.sync.dma_start(out=w4_s[32 * q : 32 * q + 8, :].bitcast(I32),
                               in_=w4_scales[:, 4 * q : 4 * q + 4, :].bitcast(I32))
         gain_t = by_row("gain_t", gain)
@@ -131,15 +118,14 @@ def tile_list_onion_neck_features_kernel(
         nc.scalar.activation(out=root[:], in_=size[:], func=ACT.Sqrt, scale=4.0)
         triple = held("triple", [P, PACK], F32)
         nc.vector.tensor_scalar(out=triple[:], in0=size[:], scalar1=3.0, scalar2=None, op0=ALU.mult)
-        if SQ_V:
-            four = held("four", [P, PACK], F32)
-            nc.vector.tensor_scalar(out=four[:], in0=size[:], scalar1=4.0, scalar2=None, op0=ALU.mult)
+        fourfold = held("fourfold", [P, PACK], F32)
+        nc.vector.tensor_scalar(out=fourfold[:], in0=size[:], scalar1=4.0, scalar2=None, op0=ALU.mult)
 
         w1_w, w1_s = [], []
         for a in range(PASSES):
             grouped = held("w1_g%d" % a, [P, PACK * H], BF16)
-            nc.scalar.copy(out=grouped[:].rearrange("p (t m j) -> p t m j", t=PACK, j=PACK),
-                           in_=w1_in[a][:].rearrange("p j (m t) -> p t m j", t=PACK))
+            nc.scalar.copy(out=grouped[:].rearrange("p (t m j) -> p m t j", t=PACK, j=PACK),
+                           in_=w1_in[a][:].rearrange("p j (m t) -> p m t j", t=PACK))
             words = held("w1_w%d" % a, [P, H], U32)
             scales = held("w1_s%d" % a, [P, H], U8)
             nc.vector.quantize_mx(out=words[:].bitcast(FP8X4), scales=scales[:], in_=grouped[:])
@@ -174,14 +160,14 @@ def tile_list_onion_neck_features_kernel(
         nc.vector.tensor_copy(out=w2_s[:].rearrange("p (t m) -> p t m", t=PACK),
                               in_=w2_s_in[:].rearrange("p (m t) -> p t m", t=PACK))
 
-        raw_sb, f_planes, f_woven, f_w, f_s, e_ps = {}, {}, {}, {}, {}, {}
+        f_planes, f_woven, f_w, f_s = {}, {}, {}, {}
         for c in range(2):
             f_planes[c] = held("f_planes%d" % c, [P, PACK, HALF], BF16)
             f_woven[c] = held("f_woven%d" % c, [P, PACK * HALF], BF16)
             f_w[c] = held("f_w%d" % c, [P, HALF], U32)
             f_s[c] = held("f_s%d" % c, [P, HALF], U8)
-        h = [rows.tile([P, S], F32, name="h%d" % t, tag="h", bufs=HB) for t in range(PACK)]
-        page = [rows.tile([P, S], F32, name="page%d" % t, tag="h", bufs=HB) for t in range(PACK)]
+        h = [rows.tile([P, S], F32, name="h%d" % t, tag="row") for t in range(PACK)]
+        page = [rows.tile([P, S], F32, name="page%d" % t, tag="row") for t in range(PACK)]
         top = held("top", [P, PACK], F32)
         opening = held("opening", [P, PACK], F32)
         bias = held("bias", [P, PACK], F32)
@@ -190,67 +176,59 @@ def tile_list_onion_neck_features_kernel(
             s = ring.tile([P, HALF], F32, name="s", tag="s")
             nc.scalar.activation(out=s[:], in_=raw_ps[c, t][:], func=ACT.Sin, scale=third[:, t : t + 1])
             sq = ring.tile([P, HALF], F32, name="sq", tag="sq")
-            if (c, t) in SQ_V:
-                nc.vector.scalar_tensor_tensor(out=sq[:], in0=s[:], scalar=four[:, t : t + 1], in1=s[:], op0=ALU.mult, op1=ALU.mult)
+            if PACK * c + t in range(0, 2 * VECTOR_SQUARES, 2):
+                nc.vector.scalar_tensor_tensor(out=sq[:], in0=s[:], scalar=fourfold[:, t : t + 1], in1=s[:],
+                                               op0=ALU.mult, op1=ALU.mult)
             else:
                 nc.scalar.activation(out=sq[:], in_=s[:], func=ACT.Square, scale=root[:, t : t + 1])
             nc.vector.scalar_tensor_tensor(out=f_planes[c][:, t, :], in0=sq[:], scalar=triple[:, t : t + 1], in1=s[:],
                                            op0=ALU.subtract, op1=ALU.mult)
 
-        def keep_raw(c, t, copy):
-            raw_sb[c, t] = held("raw%d%d" % (c, t), [P, HALF], F32)
-            copy(out=raw_sb[c, t][:], in_=raw_ps[c, t][:])
-
-        def quantise_f(c):
-            width = HALF // F_PARTS[c]
-            for i in range(F_PARTS[c]):
-                (nc.scalar.copy if (c, i) in WEAVE_S else nc.vector.tensor_copy)(out=woven(f_woven[c][:, PACK * width * i : PACK * width * (i + 1)]),
-                                      in_=weave(f_planes[c][:, :, width * i : width * (i + 1)]))
-            for i in range(F_PARTS[c]):
+        def quantise_f(c, copies):
+            width = HALF // len(copies)
+            parts = [f_woven[c][:, PACK * width * i : PACK * width * (i + 1)] for i in range(len(copies))]
+            for i, copy in enumerate(copies):
+                copy(out=woven(parts[i]), in_=weave(f_planes[c][:, :, width * i : width * (i + 1)]))
+            for i, part in enumerate(parts):
                 cols = slice(width * i, width * (i + 1))
-                nc.vector.quantize_mx(out=f_w[c][:, cols].bitcast(FP8X4), scales=f_s[c][:, cols],
-                                      in_=f_woven[c][:, PACK * width * i : PACK * width * (i + 1)])
+                nc.vector.quantize_mx(out=f_w[c][:, cols].bitcast(FP8X4), scales=f_s[c][:, cols], in_=part)
 
-        def second_product(c, t):
-            e_ps[c, t] = bank(PACK * c + t)
-            nc.tensor.matmul_mx(out=e_ps[c, t][:], lhsT=w2_w[:, 2 * P * t : 2 * P * (t + 1)].bitcast(FP4X4),
-                                lhsT_scale=w2_s[:, P * t : P * (t + 1)], rhs=f_w[c][:].bitcast(FP8X4),
-                                rhs_scale=f_s[c][:], start=True, stop=True)
-
-        def features(c, t):
-            cols = slice(HALF * c, HALF * (c + 1))
-            nc.vector.tensor_tensor(out=h[t][:, cols], in0=e_ps[c, t][:], in1=raw_sb[c, t][:], op=ALU.max)
-
+        weavers = ([nc.vector.tensor_copy], [nc.vector.tensor_copy, nc.scalar.copy])
         for c in range(2):
             for t in range(PACK):
                 sine(c, t)
-                if (c, t) in RAW_V:
-                    keep_raw(c, t, nc.vector.tensor_copy)
-            quantise_f(c)
+            quantise_f(c, weavers[c])
         nc.vector.scalar_tensor_tensor(out=opening[:], in0=slope_t[:], scalar=-1.0, in1=share_t[:], op0=ALU.mult, op1=ALU.mult)
+
+        raw_sb = {}
         for t in range(PACK):
             for c in range(2):
-                if (c, t) not in RAW_V:
-                    keep_raw(c, t, nc.scalar.copy)
+                raw_sb[c, t] = held("raw%d%d" % (c, t), [P, HALF], F32)
+                nc.scalar.copy(out=raw_sb[c, t][:], in_=raw_ps[c, t][:])
         for t in range(PACK):
             for c in range(2):
-                second_product(c, t)
-                features(c, t)
+                e_ps = bank(PACK * c + t)
+                nc.tensor.matmul_mx(out=e_ps[:], lhsT=w2_w[:, 2 * P * t : 2 * P * (t + 1)].bitcast(FP4X4),
+                                    lhsT_scale=w2_s[:, P * t : P * (t + 1)], rhs=f_w[c][:].bitcast(FP8X4),
+                                    rhs_scale=f_s[c][:], start=True, stop=True)
+                nc.vector.tensor_tensor(out=h[t][:, HALF * c : HALF * (c + 1)], in0=e_ps[:], in1=raw_sb[c, t][:], op=ALU.max)
             nc.vector.reduce_max(out=top[:, t : t + 1], in_=h[t][:], axis=AX.X)
+
         weight = held("weight", [P, PACK * L], F32, tag="f_woven1")
         for t in range(PACK):
             cols = slice(L * t, L * (t + 1))
-            (nc.gpsimd if LW_G else nc.vector).tensor_tensor(out=weight[:, cols], in0=leaf_t[:, cols], in1=wgs_t[:, cols], op=ALU.mult)
+            nc.vector.tensor_tensor(out=weight[:, cols], in0=leaf_t[:, cols], in1=wgs_t[:, cols], op=ALU.mult)
 
         w3_g = held("w3_g", [P, PACK * N], BF16)
         w3_s = held("w3_s", [P, N], U8)
         for t in range(PACK):
             nc.scalar.activation(out=bias[:, t : t + 1], in_=top[:, t : t + 1], func=ACT.Copy, scale=opening[:, t : t + 1])
-            look = keep.tile([P, L], F32, name="look%d" % t, tag="look%d" % t, align_bytes=64)
+            look = held("look%d" % t, [P, L], F32)
             nc.scalar.activation(out=look[:], in_=h[t][:].indirect(p1[:]), func=ACT.Sigmoid,
                                  bias=bias[:, t : t + 1], scale=slope_t[:, t : t + 1])
             nc.scalar.activation(out=page[t][:], in_=h[t][:], func=ACT.Copy, scale=skip_t[:, t : t + 1])
             nc.vector.tensor_tensor(out=page[t][:].indirect(p2[:]), in0=look[:], in1=weight[:, L * t : L * (t + 1)], op=ALU.mult)
+
         nc.scalar.copy(out=woven(w3_g[:]), in_=weave(w3_in[:]))
         w3_w = held("w3_w", [P, N], U32)
         nc.vector.quantize_mx(out=w3_w[:].bitcast(FP8X4), scales=w3_s[:], in_=w3_g[:])
@@ -258,10 +236,7 @@ def tile_list_onion_neck_features_kernel(
         g_planes = held("g_planes", [P, PACK, S], BF16)
         bounded = []
         for n in range(TILES):
-            if n < B_OWN:
-                tile = held("bounded%d" % n, [P, S], F32)
-            else:
-                tile = rows.tile([P, S], F32, name="bounded%d" % n, tag="h", bufs=HB)
+            tile = held("bounded%d" % n, [P, S], F32)
             for c in range(2):
                 d_ps = bank(PACK * c + n)
                 for a in range(PASSES):
@@ -270,31 +245,32 @@ def tile_list_onion_neck_features_kernel(
             bounded.append(tile)
             nc.scalar.activation(out=g_planes[:, n, :], in_=page[n][:], func=ACT.Copy, scale=gain_t[:, n : n + 1])
         last = PACK - 1
-        cut = S - M3_S
-        nc.vector.tensor_scalar(out=g_planes[:, last, :cut], in0=page[last][:, :cut], scalar1=gain_t[:, last : last + 1], scalar2=None, op0=ALU.mult)
-        if M3_S:
-            nc.scalar.activation(out=g_planes[:, last, cut:], in_=page[last][:, cut:], func=ACT.Copy, scale=gain_t[:, last : last + 1])
+        nc.vector.tensor_scalar(out=g_planes[:, last, :HALF], in0=page[last][:, :HALF], scalar1=gain_t[:, last : last + 1],
+                                scalar2=None, op0=ALU.mult)
+        nc.scalar.activation(out=g_planes[:, last, HALF:], in_=page[last][:, HALF:], func=ACT.Copy,
+                             scale=gain_t[:, last : last + 1])
 
         g_w = held("g_w", [P, S], U32)
         g_s = held("g_s", [P, S], U8)
+        y_banks = [PACK * c + n for n in (last, 0, 1) for c in range(2)]
         y_ps = {}
         quarters = S // QUARTER
         for k in range(quarters):
             c, cols = k // 2, slice(QUARTER * k, QUARTER * (k + 1))
-            g_woven = keep.tile([P, PACK * QUARTER], BF16, name="g_woven%d" % k, tag="g_woven%d" % k, align_bytes=64)
-            copy = nc.scalar.copy if k in N_S else nc.vector.tensor_copy
+            g_woven = held("g_woven%d" % k, [P, PACK * QUARTER], BF16)
+            copy = nc.scalar.copy if k == quarters - 1 else nc.vector.tensor_copy
             copy(out=woven(g_woven[:]), in_=weave(g_planes[:, :, cols]))
             nc.vector.quantize_mx(out=g_w[:, cols].bitcast(FP8X4), scales=g_s[:, cols], in_=g_woven[:])
             for n in range(TILES):
                 if k % 2 == 0:
-                    y_ps[n, c] = bank((3, 7, 0, 4, 1, 5)[TILES * c + n])
+                    y_ps[n, c] = bank(y_banks[TILES * c + n])
                 part = slice(QUARTER * (k % 2), QUARTER * (k % 2 + 1))
                 nc.tensor.matmul_mx(out=y_ps[n, c][:, part], lhsT=w3_w[:, P * n : P * (n + 1)].bitcast(FP8X4),
                                     lhsT_scale=w3_s[:, P * n : P * (n + 1)], rhs=g_w[:, cols].bitcast(FP8X4),
                                     rhs_scale=g_s[:, cols], start=True, stop=True)
         for c in range(2):
             half = slice(HALF * c, HALF * (c + 1))
-            result = keep.tile([P, TILES, HALF], F32, name="result%d" % c, tag="g_woven%d" % RES[c], align_bytes=64)
+            result = held("result%d" % c, [P, TILES, HALF], F32, tag="g_woven%d" % (2 * c + 1))
             for n in range(TILES):
                 nc.vector.tensor_tensor(out=result[:, n, :], in0=y_ps[n, c][:], in1=bounded[n][:, half], op=ALU.max)
                 nc.sync.dma_start(out=out[P * n : P * (n + 1), half], in_=result[:, n, :])

from contextlib import ExitStack

import concourse.mybir as mybir

K, T, S, L, H, N = 1024, 4096, 1024, 512, 512, 384
FLOPS = 2 * S * (K * H + H * H + H * N + K * N)

F32 = mybir.dt.float32
BF16 = mybir.dt.bfloat16
I32 = mybir.dt.int32
U32 = mybir.dt.uint32
U16 = mybir.dt.uint16
U8 = mybir.dt.uint8
FP8X4 = mybir.dt.float8_e4m3fn_x4
FP4X4 = mybir.dt.float4_e2m1fn_x4
ALU = mybir.AluOpType
ACT = mybir.ActivationFunctionType
AX = mybir.AxisListType

P = 128
PACK = 4
HALF = 512
QUARTER = 256
PASSES = K // (P * PACK)
TILES = N // P
QUADRANTS = 4
SINE_BUFS = 4
ROW_BUFS = PACK + 1
VECTOR_SQUARES = 3


def weave(src):
    return src.rearrange("p t (c i) -> p c t i", i=4)


def woven(dst):
    return dst.rearrange("p (c i t) -> p c t i", i=4, t=PACK)


def tile_list_onion_neck_features_kernel(
    tc, tab_words, tab_scales, offs, pos1, pos2, w1, w2_words, w2_scales, w3, w4_words, w4_scales,
    swing, slope, share, leaf, skip, wgs, gain, out,
):
    nc = tc.nc
    with ExitStack() as ctx:
        lists = ctx.enter_context(tc.tile_pool(name="lists", bufs=1))
        keep = ctx.enter_context(tc.tile_pool(name="keep", bufs=1))
        ring = ctx.enter_context(tc.tile_pool(name="ring", bufs=SINE_BUFS))
        rows = ctx.enter_context(tc.tile_pool(name="rows", bufs=ROW_BUFS))
        psum = ctx.enter_context(tc.psum_pool(name="psum", bufs=1))

        def held(name, shape, dtype, tag=None):
            return keep.tile(shape, dtype, name=name, tag=tag or name, align_bytes=64)

        def bank(b):
            return psum.tile([P, HALF], F32, name="bank%d" % b, tag="bank%d" % b)

        def by_row(name, vec):
            tile = held(name, [P, PACK], F32)
            nc.sync.dma_start(out=tile[:], in_=vec.rearrange("(p t) -> p t", t=PACK))
            return tile

        idx = lists.tile([P, S // 16], U16, name="idx")
        p1 = lists.tile([P, L // 16], U16, name="p1")
        p2 = lists.tile([P, L // 16], U16, name="p2")
        tab_s = held("tab_s", [P, T], U8)
        nc.vector.memset(tab_s[:].bitcast(I32), 0)
        w2_s_in = held("w2_s_in", [P, H], U8)
        nc.vector.memset(w2_s_in[:].bitcast(I32), 0)
        w4_s = held("w4_s", [P, N], U8)
        nc.vector.memset(w4_s[:].bitcast(I32), 0)

        w1_in = [held("w1_in%d" % a, [P, PACK, H], F32) for a in range(PASSES)]
        tab_w = [held("tab_w%d" % a, [P, T], U32) for a in range(PASSES)]

        def load_w1(a):
            nc.sync.dma_start(out=w1_in[a][:], in_=w1[512 * a : 512 * (a + 1), :].rearrange("(p j) c -> p j c", j=PACK))

        nc.sync.dma_start(idx[:], offs)
        swing_t = by_row("swing_t", swing)
        load_w1(0)
        for q in range(QUADRANTS):
            nc.gpsimd.dma_start(out=tab_s[32 * q : 32 * q + 8, :].bitcast(I32),
                                in_=tab_scales[:, 4 * q : 4 * q + 4, :].bitcast(I32))
        w2_in = held("w2_in", [P, 2 * H], U8)
        nc.sync.dma_start(out=w2_in[:].bitcast(I32), in_=w2_words[0].bitcast(I32))
        load_w1(1)
        for a in range(PASSES):
            nc.sync.dma_start(out=tab_w[a][:].bitcast(I32), in_=tab_words[a].rearrange("p c i -> p (c i)").bitcast(I32))
        for q in range(QUADRANTS):
            nc.sync.dma_start(out=w2_s_in[32 * q : 32 * q + 4, :].bitcast(I32),
                              in_=w2_scales[0, 4 * q : 4 * q + 4, :].bitcast(I32))
        slope_t = by_row("slope_t", slope)
        share_t = by_row("share_t", share)
        leaf_t = held("leaf_t", [P, PACK * L], F32)
        nc.sync.dma_start(out=leaf_t[:], in_=leaf.rearrange("(p t) m -> p (t m)", t=PACK))
        wgs_t = held("wgs_t", [P, PACK * L], F32)
        for q in (0, 2, 1, 3):
            nc.sync.dma_start(out=wgs_t[32 * q : 32 * (q + 1), :], in_=wgs.rearrange("(p t) m -> p (t m)", t=PACK))
        skip_t = by_row("skip_t", skip)
        nc.sync.dma_start(p1[:], pos1)
        nc.sync.dma_start(p2[:], pos2)
        w3_in = held("w3_in", [P, PACK, N], F32)
        nc.sync.dma_start(out=w3_in[:], in_=w3.rearrange("(p j) c -> p j c", j=PACK))
        w4_w = held("w4_w", [P, PASSES, N], U32)
        nc.sync.dma_start(out=w4_w[:].bitcast(I32), in_=w4_words.rearrange("a p c i -> p a (c i)").bitcast(I32))
        for q in range(QUADRANTS):
            nc.sync.dma_start(out=w4_s[32 * q : 32 * q + 8, :].bitcast(I32),
                              in_=w4_scales[:, 4 * q : 4 * q + 4, :].bitcast(I32))
        gain_t = by_row("gain_t", gain)

        third = held("third", [P, PACK], F32)
        nc.vector.tensor_scalar(out=third[:], in0=swing_t[:], scalar1=0.0, scalar2=None, op0=ALU.is_ge)
        size = held("size", [P, PACK], F32)
        nc.vector.scalar_tensor_tensor(out=size[:], in0=swing_t[:], scalar=-1.0, in1=swing_t[:], op0=ALU.mult, op1=ALU.max)
        nc.vector.tensor_scalar(out=third[:], in0=third[:], scalar1=-2.0 / 3.0, scalar2=1.0 / 3.0, op0=ALU.mult, op1=ALU.add)
        root = held("root", [P, PACK], F32)
        nc.scalar.activation(out=root[:], in_=size[:], func=ACT.Sqrt, scale=4.0)
        triple = held("triple", [P, PACK], F32)
        nc.vector.tensor_scalar(out=triple[:], in0=size[:], scalar1=3.0, scalar2=None, op0=ALU.mult)
        fourfold = held("fourfold", [P, PACK], F32)
        nc.vector.tensor_scalar(out=fourfold[:], in0=size[:], scalar1=4.0, scalar2=None, op0=ALU.mult)

        w1_w, w1_s = [], []
        for a in range(PASSES):
            grouped = held("w1_g%d" % a, [P, PACK * H], BF16)
            nc.scalar.copy(out=grouped[:].rearrange("p (t m j) -> p m t j", t=PACK, j=PACK),
                           in_=w1_in[a][:].rearrange("p j (m t) -> p m t j", t=PACK))
            words = held("w1_w%d" % a, [P, H], U32)
            scales = held("w1_s%d" % a, [P, H], U8)
            nc.vector.quantize_mx(out=words[:].bitcast(FP8X4), scales=scales[:], in_=grouped[:])
            w1_w.append(words)
            w1_s.append(scales)

        v_s = held("v_s", [P, S], U8)
        nc.vector.tensor_copy(out=v_s[:], in_=tab_s[:].indirect(idx[:]))
        v_w = {}

        def gather(a, c):
            tile = held("v_w%d%d" % (a, c), [P, HALF], U32)
            nc.vector.tensor_copy(out=tile[:], in_=tab_w[a][:].indirect(idx[:, 32 * c : 32 * (c + 1)]))
            v_w[a, c] = tile

        def on_table(acc, words, scales, a, c):
            nc.tensor.matmul_mx(out=acc[:], lhsT=words.bitcast(FP8X4), lhsT_scale=scales,
                                rhs=v_w[a, c][:].bitcast(FP8X4), rhs_scale=v_s[4 * a : P, HALF * c : HALF * (c + 1)],
                                start=(a == 0), stop=(a == PASSES - 1))

        raw_ps = {(c, t): bank(PACK * c + t) for c in range(2) for t in range(PACK)}
        for a in range(PASSES):
            for c in range(2):
                gather(a, c)
                for t in range(PACK):
                    on_table(raw_ps[c, t], w1_w[a][:, P * t : P * (t + 1)], w1_s[a][:, P * t : P * (t + 1)], a, c)

        w2_w = held("w2_w", [P, 2 * H], U8)
        nc.vector.tensor_copy(out=w2_w[:].rearrange("p (t m b) -> p t m b", t=PACK, b=2),
                              in_=w2_in[:].rearrange("p (m t b) -> p t m b", t=PACK, b=2))
        w2_s = held("w2_s", [P, H], U8)
        nc.vector.tensor_copy(out=w2_s[:].rearrange("p (t m) -> p t m", t=PACK),
                              in_=w2_s_in[:].rearrange("p (m t) -> p t m", t=PACK))

        f_planes, f_woven, f_w, f_s = {}, {}, {}, {}
        for c in range(2):
            f_planes[c] = held("f_planes%d" % c, [P, PACK, HALF], BF16)
            f_woven[c] = held("f_woven%d" % c, [P, PACK * HALF], BF16)
            f_w[c] = held("f_w%d" % c, [P, HALF], U32)
            f_s[c] = held("f_s%d" % c, [P, HALF], U8)
        h = [rows.tile([P, S], F32, name="h%d" % t, tag="row") for t in range(PACK)]
        page = [rows.tile([P, S], F32, name="page%d" % t, tag="row") for t in range(PACK)]
        top = held("top", [P, PACK], F32)
        opening = held("opening", [P, PACK], F32)
        bias = held("bias", [P, PACK], F32)

        def sine(c, t):
            s = ring.tile([P, HALF], F32, name="s", tag="s")
            nc.scalar.activation(out=s[:], in_=raw_ps[c, t][:], func=ACT.Sin, scale=third[:, t : t + 1])
            sq = ring.tile([P, HALF], F32, name="sq", tag="sq")
            if PACK * c + t in range(0, 2 * VECTOR_SQUARES, 2):
                nc.vector.scalar_tensor_tensor(out=sq[:], in0=s[:], scalar=fourfold[:, t : t + 1], in1=s[:],
                                               op0=ALU.mult, op1=ALU.mult)
            else:
                nc.scalar.activation(out=sq[:], in_=s[:], func=ACT.Square, scale=root[:, t : t + 1])
            nc.vector.scalar_tensor_tensor(out=f_planes[c][:, t, :], in0=sq[:], scalar=triple[:, t : t + 1], in1=s[:],
                                           op0=ALU.subtract, op1=ALU.mult)

        def quantise_f(c, copies):
            width = HALF // len(copies)
            parts = [f_woven[c][:, PACK * width * i : PACK * width * (i + 1)] for i in range(len(copies))]
            for i, copy in enumerate(copies):
                copy(out=woven(parts[i]), in_=weave(f_planes[c][:, :, width * i : width * (i + 1)]))
            for i, part in enumerate(parts):
                cols = slice(width * i, width * (i + 1))
                nc.vector.quantize_mx(out=f_w[c][:, cols].bitcast(FP8X4), scales=f_s[c][:, cols], in_=part)

        weavers = ([nc.vector.tensor_copy], [nc.vector.tensor_copy, nc.scalar.copy])
        for c in range(2):
            for t in range(PACK):
                sine(c, t)
            quantise_f(c, weavers[c])
        nc.vector.scalar_tensor_tensor(out=opening[:], in0=slope_t[:], scalar=-1.0, in1=share_t[:], op0=ALU.mult, op1=ALU.mult)

        raw_sb = {}
        for t in range(PACK):
            for c in range(2):
                raw_sb[c, t] = held("raw%d%d" % (c, t), [P, HALF], F32)
                nc.scalar.copy(out=raw_sb[c, t][:], in_=raw_ps[c, t][:])
        for t in range(PACK):
            for c in range(2):
                e_ps = bank(PACK * c + t)
                nc.tensor.matmul_mx(out=e_ps[:], lhsT=w2_w[:, 2 * P * t : 2 * P * (t + 1)].bitcast(FP4X4),
                                    lhsT_scale=w2_s[:, P * t : P * (t + 1)], rhs=f_w[c][:].bitcast(FP8X4),
                                    rhs_scale=f_s[c][:], start=True, stop=True)
                nc.vector.tensor_tensor(out=h[t][:, HALF * c : HALF * (c + 1)], in0=e_ps[:], in1=raw_sb[c, t][:], op=ALU.max)
            nc.vector.reduce_max(out=top[:, t : t + 1], in_=h[t][:], axis=AX.X)

        weight = held("weight", [P, PACK * L], F32, tag="f_woven1")
        for t in range(PACK):
            cols = slice(L * t, L * (t + 1))
            nc.vector.tensor_tensor(out=weight[:, cols], in0=leaf_t[:, cols], in1=wgs_t[:, cols], op=ALU.mult)

        w3_g = held("w3_g", [P, PACK * N], BF16)
        w3_s = held("w3_s", [P, N], U8)
        for t in range(PACK):
            nc.scalar.activation(out=bias[:, t : t + 1], in_=top[:, t : t + 1], func=ACT.Copy, scale=opening[:, t : t + 1])
            look = held("look%d" % t, [P, L], F32)
            nc.scalar.activation(out=look[:], in_=h[t][:].indirect(p1[:]), func=ACT.Sigmoid,
                                 bias=bias[:, t : t + 1], scale=slope_t[:, t : t + 1])
            nc.scalar.activation(out=page[t][:], in_=h[t][:], func=ACT.Copy, scale=skip_t[:, t : t + 1])
            nc.vector.tensor_tensor(out=page[t][:].indirect(p2[:]), in0=look[:], in1=weight[:, L * t : L * (t + 1)], op=ALU.mult)

        nc.scalar.copy(out=woven(w3_g[:]), in_=weave(w3_in[:]))
        w3_w = held("w3_w", [P, N], U32)
        nc.vector.quantize_mx(out=w3_w[:].bitcast(FP8X4), scales=w3_s[:], in_=w3_g[:])

        g_planes = held("g_planes", [P, PACK, S], BF16)
        bounded = []
        for n in range(TILES):
            tile = held("bounded%d" % n, [P, S], F32)
            for c in range(2):
                d_ps = bank(PACK * c + n)
                for a in range(PASSES):
                    on_table(d_ps, w4_w[:, a, P * n : P * (n + 1)], w4_s[4 * a : P, P * n : P * (n + 1)], a, c)
                nc.scalar.activation(out=tile[:, HALF * c : HALF * (c + 1)], in_=d_ps[:], func=ACT.Tanh)
            bounded.append(tile)
            nc.scalar.activation(out=g_planes[:, n, :], in_=page[n][:], func=ACT.Copy, scale=gain_t[:, n : n + 1])
        last = PACK - 1
        nc.vector.tensor_scalar(out=g_planes[:, last, :HALF], in0=page[last][:, :HALF], scalar1=gain_t[:, last : last + 1],
                                scalar2=None, op0=ALU.mult)
        nc.scalar.activation(out=g_planes[:, last, HALF:], in_=page[last][:, HALF:], func=ACT.Copy,
                             scale=gain_t[:, last : last + 1])

        g_w = held("g_w", [P, S], U32)
        g_s = held("g_s", [P, S], U8)
        y_banks = [PACK * c + n for n in (last, 0, 1) for c in range(2)]
        y_ps = {}
        quarters = S // QUARTER
        for k in range(quarters):
            c, cols = k // 2, slice(QUARTER * k, QUARTER * (k + 1))
            g_woven = held("g_woven%d" % k, [P, PACK * QUARTER], BF16)
            copy = nc.scalar.copy if k == quarters - 1 else nc.vector.tensor_copy
            copy(out=woven(g_woven[:]), in_=weave(g_planes[:, :, cols]))
            nc.vector.quantize_mx(out=g_w[:, cols].bitcast(FP8X4), scales=g_s[:, cols], in_=g_woven[:])
            for n in range(TILES):
                if k % 2 == 0:
                    y_ps[n, c] = bank(y_banks[TILES * c + n])
                part = slice(QUARTER * (k % 2), QUARTER * (k % 2 + 1))
                nc.tensor.matmul_mx(out=y_ps[n, c][:, part], lhsT=w3_w[:, P * n : P * (n + 1)].bitcast(FP8X4),
                                    lhsT_scale=w3_s[:, P * n : P * (n + 1)], rhs=g_w[:, cols].bitcast(FP8X4),
                                    rhs_scale=g_s[:, cols], start=True, stop=True)
        for c in range(2):
            half = slice(HALF * c, HALF * (c + 1))
            result = held("result%d" % c, [P, TILES, HALF], F32, tag="g_woven%d" % (2 * c + 1))
            for n in range(TILES):
                nc.vector.tensor_tensor(out=result[:, n, :], in0=y_ps[n, c][:], in1=bounded[n][:, half], op=ALU.max)
                nc.sync.dma_start(out=out[P * n : P * (n + 1), half], in_=result[:, n, :])
